import numpy as np
import ml_dtypes


def mxq(x, axis, fmt="e4m3"):
    dtype, down = {"e4m3": (ml_dtypes.float8_e4m3fn, 7), "e5m2": (ml_dtypes.float8_e5m2, 14)}[fmt]
    v = np.moveaxis(np.asarray(x, np.float32).astype(ml_dtypes.bfloat16).astype(np.float64), axis, -1)
    blocks = v.reshape(v.shape[:-1] + (-1, 32))
    amax = np.abs(blocks).max(-1, keepdims=True)
    byte = np.maximum(np.where(amax > 0, np.frexp(amax)[1] - 1 + 127, 0) - down, 1)
    scale = np.exp2(byte - 127.0)
    codes = (blocks / scale).astype(np.float32).astype(dtype).astype(np.float64)
    return np.moveaxis((codes * scale).reshape(v.shape), -1, axis)


WIDE = False


def mx_kscale(k):
    if not WIDE:
        return np.ones(k)
    levels = np.array([10, -10, 5, -5, 0])
    if k % 512:
        return np.exp2(np.random.permutation(np.resize(levels, k // 32))).repeat(32)
    a = np.empty((k // 512, 16))
    for p in range(k // 512):
        a[p, :8] = np.random.permutation(np.resize(levels, 8))
        for g in range(8):
            far = levels[np.abs(levels - a[p, g]) >= 10]
            a[p, g + 8] = far[np.random.randint(len(far))]
    return np.exp2(a.ravel()).repeat(32)


def f64(x):
    return np.asarray(x).astype(np.float64)


def striped(idx):
    return np.tile(idx.reshape(-1, 16).T, (8, 1)).astype(np.uint16)


def unstriped(offs):
    return offs[:16].T.reshape(-1).astype(np.int64)


def striped8(idx):
    return np.concatenate([x.reshape(-1, 16).T for x in idx]).astype(np.uint16)


def runs(offs, k):
    lists = np.stack([offs[16 * r : 16 * r + 16].T.reshape(-1) for r in range(8)]).astype(np.int64)
    return lists[np.arange(k) % 512 // 64]


def pack_weight(w):
    k, n = w.shape
    w = f64(np.asarray(w, np.float32).astype(ml_dtypes.bfloat16)).reshape(k // 32, 32, n)
    amax = np.abs(w).max(1)
    byte = np.clip(np.where(amax > 0, np.frexp(amax)[1] - 1 + 127 - 7, 1), 1, 254)
    scaled = (w * np.exp2(127.0 - byte)[:, None, :]).reshape(k, n).astype(np.float32)
    words = np.ascontiguousarray(scaled.reshape(k // 512, 128, 4, n).transpose(0, 1, 3, 2)).astype(ml_dtypes.float8_e4m3fn).view(np.uint8)
    return words, np.ascontiguousarray(byte.astype(np.uint8).reshape(k // 512, 16, n))


def unpack_weight(words, scales):
    g, p, n, _ = words.shape
    vals = np.ascontiguousarray(words).view(ml_dtypes.float8_e4m3fn).astype(np.float64) * np.repeat(np.exp2(scales.astype(np.float64) - 127.0), 8, axis=1)[..., None]
    return vals.transpose(0, 1, 3, 2).reshape(g * 512, n)


E2M1 = np.array([0.0, 0.5, 1.0, 1.5, 2.0, 3.0, 4.0, 6.0, -0.0, -0.5, -1.0, -1.5, -2.0, -3.0, -4.0, -6.0])


def pack_fp4(w):
    k, n = w.shape
    w = f64(np.asarray(w, np.float32).astype(ml_dtypes.bfloat16)).reshape(k // 32, 32, n)
    amax = np.abs(w).max(1)
    mant, ex = np.frexp(amax / 6.0)
    byte = np.clip(np.where(amax > 0, np.where(mant > 0.5, ex, ex - 1) + 127, 1), 1, 254)
    scaled = (w * np.exp2(127.0 - byte)[:, None, :]).reshape(k, n).astype(np.float32)
    c = np.ascontiguousarray(scaled.reshape(k // 512, 128, 4, n).transpose(0, 1, 3, 2)).astype(ml_dtypes.float4_e2m1fn).view(np.uint8) & 0xF
    words = (c[..., 0::2] | (c[..., 1::2] << 4)).reshape(k // 512, 128, 2 * n)
    return np.ascontiguousarray(words), np.ascontiguousarray(byte.astype(np.uint8).reshape(k // 512, 16, n))


def unpack_fp4(words, scales):
    g, _, n = scales.shape
    words = np.ascontiguousarray(words).reshape(g, 128, n, 2)
    nib = np.empty((g, 128, n, 4), np.uint8)
    nib[..., 0::2] = words & 0xF
    nib[..., 1::2] = words >> 4
    vals = E2M1[nib] * np.repeat(np.exp2(scales.astype(np.float64) - 127.0), 8, axis=1)[..., None]
    return vals.transpose(0, 1, 3, 2).reshape(g * 512, n)


def sigmoid(v):
    return 1.0 / (1.0 + np.exp(-np.maximum(v, -700.0)))

def planes(y):
    n, m = y.shape
    v = y.astype(np.float32).astype(ml_dtypes.bfloat16).astype(np.float64).reshape(n // 32, 32, m)
    top = np.abs(v).max(1)
    byte = np.clip(np.where(top > 0, np.frexp(top)[1] - 1 + 127 - 7, 1), 1, 254)
    codes = (v * np.exp2(127.0 - byte)[:, None, :]).reshape(n, m).astype(np.float32).astype(ml_dtypes.float8_e4m3fn).view(np.uint8)
    words = codes.reshape(n // 512, 128, 4, m).transpose(0, 1, 3, 2)
    return np.ascontiguousarray(words), np.ascontiguousarray(byte.astype(np.uint8).reshape(n // 512, 16, m))


K, T, S, V, N, H = 512, 2048, 1024, 512, 512, 512


def setup_inputs():
    n = np.random.standard_normal
    s = mx_kscale(K)[:, None]
    u = mx_kscale(H)
    packed_xT = pack_weight(n((K, T)) * s)
    packed_w1 = pack_fp4(n((K, H)) / np.sqrt(K) / s)
    packed_w3 = pack_fp4(n((H, N)) / np.sqrt(H) / u[:, None])
    return {
        "x_words": packed_xT[0],
        "x_scales": packed_xT[1],
        "w1_words": packed_w1[0],
        "w1_scales": packed_w1[1],
        "w2": (n((K, H)) / np.sqrt(K) / s * u).astype(np.float32),
        "w3_words": packed_w3[0],
        "w3_scales": packed_w3[1],
        "offs": striped(np.random.permutation(T)[:S]),
        "left": striped8(np.stack([np.random.permutation(S)[:V] for _ in range(8)])),
        "right": striped8(np.stack([np.random.permutation(S)[:V] for _ in range(8)])),
    }


def reference(x_words, x_scales, w1_words, w1_scales, w2, w3_words, w3_scales, offs, left, right):
    xq = unpack_weight(x_words, x_scales)[:, unstriped(offs)]
    val = mxq(f64(w2), 0, "e4m3").T @ xq
    vr = val[np.arange(H)[:, None], runs(right, H)]
    s = unpack_fp4(w1_words, w1_scales).T @ xq
    q = sigmoid(s[np.arange(H)[:, None], runs(left, H)] - (s[np.arange(H)[:, None], runs(right, H)]))
    z = vr + q * (val[np.arange(H)[:, None], runs(left, H)] - vr)
    out_0 = unpack_fp4(w3_words, w3_scales).T @ mxq(z, 0, "e4m3")
    return (out_0,) + planes(out_0)

@@ -1,0 +1,244 @@
+from contextlib import ExitStack
+
+import concourse.mybir as mybir
+
+K, T, S, V, N, H = 512, 2048, 1024, 512, 512, 512
+FLOPS = 2 * K * H * S * 2 + 2 * H * N * V
+
+F32 = mybir.dt.float32
+BF16 = mybir.dt.bfloat16
+I32 = mybir.dt.int32
+U32 = mybir.dt.uint32
+U16 = mybir.dt.uint16
+U8 = mybir.dt.uint8
+FP8X4 = mybir.dt.float8_e4m3fn_x4
+FP4X4 = mybir.dt.float4_e2m1fn_x4
+ALU = mybir.AluOpType
+SIGMOID = mybir.ActivationFunctionType.Sigmoid
+
+P = 128
+PACK = 4
+GROUP = 16
+HALF = 512
+CHUNKS = (256, 128, 128)
+OUT_COLS = 128
+
+
+def load_scale_rows(queue, plane, scales):
+    for quad in range(4):
+        queue.dma_start(
+            out=plane[32 * quad : 32 * quad + 4, :].bitcast(I32),
+            in_=scales[0, 4 * quad : 4 * quad + 4, :].bitcast(I32),
+        )
+
+
+def deal_fp4_words(nc, dealt, raw):
+    nc.vector.tensor_copy(
+        out=dealt[:].rearrange("p (t m b) -> p t m b", t=PACK, b=2),
+        in_=raw[:].rearrange("p (m t b) -> p t m b", t=PACK, b=2),
+    )
+
+
+def deal_scale_bytes(nc, dealt, raw):
+    nc.vector.tensor_copy(
+        out=dealt[:].rearrange("p (t m) -> p t m", t=PACK),
+        in_=raw[:].rearrange("p (m t) -> p t m", t=PACK),
+    )
+
+
+def tile_picked_tourney_none_po_kernel(
+    tc, x_words, x_scales, w1_words, w1_scales, w2, w3_words, w3_scales, offs, left, right, out_0, out_1, out_2
+):
+    nc = tc.nc
+    with ExitStack() as ctx:
+        keep = ctx.enter_context(tc.tile_pool(name="keep", bufs=1))
+        acc_pool = ctx.enter_context(tc.psum_pool(name="acc", bufs=6))
+        out_pool = ctx.enter_context(tc.psum_pool(name="outp", bufs=2))
+
+        offs_sb = keep.tile([P, S // GROUP], U16, name="offs_sb")
+        left_sb = keep.tile([P, V // GROUP], U16, name="left_sb")
+        right_sb = keep.tile([P, V // GROUP], U16, name="right_sb")
+        xs_all = keep.tile([P, T], U8, name="xs_all", tag="slot_a", align_bytes=64)
+        xw_all = keep.tile([P, T], I32, name="xw_all", align_bytes=64)
+        w1_raw = keep.tile([P, 2 * H], U8, name="w1_raw", tag="slot_w", align_bytes=64)
+        w1s_raw = keep.tile([P, H], U8, name="w1s_raw", align_bytes=64)
+        warm = keep.tile([P, 2], F32, name="warm")
+
+        nc.vector.memset(xs_all[:].bitcast(I32), 0)
+        nc.vector.memset(w1s_raw[:].bitcast(I32), 0)
+        nc.vector.memset(warm[:, 0:1], 0.0)
+
+        nc.sync.dma_start(offs_sb[:], offs)
+        load_scale_rows(nc.scalar, xs_all, x_scales)
+        nc.sync.dma_start(right_sb[:], right)
+        nc.sync.dma_start(left_sb[:], left)
+        nc.sync.dma_start(out=w1_raw[:].bitcast(I32), in_=w1_words[0].bitcast(I32))
+        nc.sync.dma_start(out=xw_all[:], in_=x_words[0].rearrange("p n t -> p (n t)").bitcast(I32))
+        load_scale_rows(nc.scalar, w1s_raw, w1_scales)
+        nc.scalar.activation(warm[:, 1:2], warm[:, 0:1], SIGMOID)
+
+        xs = keep.tile([P, S], U8, name="xs", align_bytes=64)
+        nc.vector.tensor_copy(xs[:], xs_all[:].indirect(offs_sb[:]))
+        w1q = keep.tile([P, 2 * H], U8, name="w1q", tag="slot_b", align_bytes=64)
+        w1s = keep.tile([P, H], U8, name="w1s", align_bytes=64)
+        w3q = keep.tile([P, 2 * N], U8, name="w3q", align_bytes=64)
+        w3s = keep.tile([P, N], U8, name="w3s", align_bytes=64)
+        deal_fp4_words(nc, w1q, w1_raw)
+        w3_raw = keep.tile([P, 2 * N], U8, name="w3_raw", tag="slot_w", align_bytes=64)
+        nc.sync.dma_start(out=w3_raw[:].bitcast(I32), in_=w3_words[0].bitcast(I32))
+        w2_raw = keep.tile([P, PACK, H], F32, name="w2_raw", tag="slot_a", align_bytes=64)
+        nc.sync.dma_start(out=w2_raw[:], in_=w2.rearrange("(p j) c -> p j c", j=PACK))
+        xw = []
+        for h in range(S // HALF):
+            xw_h = keep.tile([P, HALF], U32, name=f"xw{h}", align_bytes=64)
+            nc.vector.tensor_copy(
+                xw_h[:], xw_all[:].bitcast(U32).indirect(offs_sb[:, h * HALF // GROUP : (h + 1) * HALF // GROUP])
+            )
+            xw.append(xw_h)
+            if h == 0:
+                deal_scale_bytes(nc, w1s, w1s_raw)
+        load_scale_rows(nc.sync, w1s_raw, w3_scales)
+        deal_fp4_words(nc, w3q, w3_raw)
+        deal_scale_bytes(nc, w3s, w1s_raw)
+
+        def multiply(lhs, lhs_scale):
+            banks = []
+            for h in range(S // HALF):
+                cols = slice(h * HALF, (h + 1) * HALF)
+                acc = acc_pool.tile([P, HALF], F32, name="acc")
+                nc.tensor.matmul_mx(
+                    out=acc[:], lhsT=lhs, lhsT_scale=lhs_scale,
+                    rhs=xw[h][:].bitcast(FP8X4), rhs_scale=xs[:, cols], start=True, stop=True,
+                )
+                banks.append(acc)
+            return banks
+
+        def evacuate(name, banks):
+            rows = keep.tile([P, S], F32, name=name, align_bytes=64)
+            for h, acc in enumerate(banks):
+                nc.scalar.copy(rows[:, h * HALF : (h + 1) * HALF], acc[:])
+            return rows
+
+        s_acc = [
+            multiply(w1q[:, 2 * P * t : 2 * P * (t + 1)].bitcast(FP4X4), w1s[:, P * t : P * (t + 1)])
+            for t in range(3)
+        ]
+        s_rows = [evacuate(f"s{t}", s_acc[t]) for t in range(3)]
+        s_acc3 = multiply(w1q[:, 2 * P * 3 : 2 * P * 4].bitcast(FP4X4), w1s[:, P * 3 : P * 4])
+
+        w2b = keep.tile([P, H * PACK], BF16, name="w2b", tag="slot_b", align_bytes=64)
+        w2b_v = w2b[:].rearrange("p (t m j) -> p m j t", t=PACK, j=PACK)
+        w2_v = w2_raw[:].rearrange("p j (m t) -> p m j t", t=PACK)
+        nc.scalar.copy(w2b_v, w2_v)
+        s_rows.append(evacuate("s3", s_acc3))
+        w2q = keep.tile([P, H], U32, name="w2q", align_bytes=64)
+        w2s = keep.tile([P, H], U8, name="w2s", align_bytes=64)
+
+        s_right = [keep.tile([P, V], F32, name=f"sr{t}") for t in range(3)]
+        diff = [keep.tile([P, V], F32, name=f"d{t}") for t in range(PACK)]
+        q_all = keep.tile([P, 2 * PACK, V], F32, name="q_all", tag="slot_a", align_bytes=64)
+        q_left = [q_all[:, 2 * t, :] for t in range(PACK)]
+        q_right = [q_all[:, 2 * t + 1, :] for t in range(PACK)]
+
+        def fetch_right(t):
+            nc.vector.tensor_copy(s_right[t][:], s_rows[t][:].indirect(right_sb[:]))
+
+        def fetch_left(t):
+            nc.vector.tensor_tensor(diff[t][:], s_rows[t][:].indirect(left_sb[:]), s_right[t][:], ALU.subtract)
+
+        def gates(t, cols):
+            nc.scalar.activation(q_left[t][:, cols], diff[t][:, cols], SIGMOID)
+            nc.scalar.activation(q_right[t][:, cols], diff[t][:, cols], SIGMOID, scale=-1.0)
+
+        fetch_right(0)
+        fetch_right(1)
+        fetch_left(0)
+        fetch_right(2)
+        fetch_left(1)
+        nc.vector.quantize_mx(out=w2q[:].bitcast(FP8X4), scales=w2s[:], in_=w2b[:])
+        s_right.append(keep.tile([P, V], F32, name="sr3", tag="slot_b", align_bytes=64))
+        fetch_right(3)
+        fetch_left(2)
+        fetch_left(3)
+
+        val_rows = []
+        first, rest = slice(0, CHUNKS[0]), slice(CHUNKS[0], V)
+        gates(0, slice(0, V))
+        gates(1, slice(0, V))
+        for t in range(PACK):
+            banks = multiply(w2q[:, P * t : P * (t + 1)].bitcast(FP8X4), w2s[:, P * t : P * (t + 1)])
+            val_rows.append(evacuate(f"val{t}", banks))
+            if t >= 2:
+                gates(t, first)
+        gates(2, rest)
+        gates(3, rest)
+
+        yq = keep.tile([P, V], U32, name="yq", align_bytes=64)
+        ys = keep.tile([P, V], U8, name="ys", align_bytes=64)
+        out_rows = out_0.rearrange("(p t) v -> p t v", t=PACK)
+        out_words = out_1[0].rearrange("p n t -> p (n t)").bitcast(I32)
+
+        def mix(c, v0, n):
+            part_l = keep.tile([P, PACK, n], F32, name=f"pl{c}")
+            part_r = keep.tile([P, PACK, n], F32, name=f"pr{c}")
+            lst = slice(v0 // GROUP, (v0 + n) // GROUP)
+            for t in range(PACK):
+                nc.vector.tensor_tensor(
+                    part_l[:, t, :], val_rows[t][:].indirect(left_sb[:, lst]), q_left[t][:, v0 : v0 + n], ALU.mult
+                )
+                nc.vector.tensor_tensor(
+                    part_r[:, t, :], val_rows[t][:].indirect(right_sb[:, lst]), q_right[t][:, v0 : v0 + n], ALU.mult
+                )
+            zb = keep.tile([P, n * PACK], BF16, name=f"zb{c}", align_bytes=64)
+            nc.vector.tensor_tensor(
+                zb[:].rearrange("p (c i t) -> p c t i", i=4, t=PACK),
+                part_l[:].rearrange("p t (c i) -> p c t i", i=4),
+                part_r[:].rearrange("p t (c i) -> p c t i", i=4),
+                ALU.add,
+            )
+            return zb
+
+        def quantize_z(c, zb, n):
+            zq = keep.tile([P, n], U32, name=f"zq{c}", align_bytes=64)
+            zs = keep.tile([P, n], U8, name=f"zs{c}", align_bytes=64)
+            nc.vector.quantize_mx(out=zq[:].bitcast(FP8X4), scales=zs[:], in_=zb[:])
+            return zq, zs
+
+        def out_layer(zq, zs, z0, v0):
+            acc = out_pool.tile([P, PACK, OUT_COLS], F32, name="yacc")
+            for t in range(PACK):
+                nc.tensor.matmul_mx(
+                    out=acc[:, t, :],
+                    lhsT=w3q[:, 2 * P * t : 2 * P * (t + 1)].bitcast(FP4X4), lhsT_scale=w3s[:, P * t : P * (t + 1)],
+                    rhs=zq[:, z0 : z0 + OUT_COLS].bitcast(FP8X4), rhs_scale=zs[:, z0 : z0 + OUT_COLS],
+                    start=True, stop=True,
+                )
+            yb = keep.tile([P, OUT_COLS * PACK], BF16, name=f"yb{v0}", align_bytes=64)
+            nc.scalar.copy(yb[:].rearrange("p (n t) -> p n t", t=PACK), acc[:].rearrange("p t n -> p n t"))
+            y = keep.tile([P, PACK, OUT_COLS], F32, name=f"y{v0}")
+            nc.scalar.copy(y[:], acc[:])
+            nc.sync.dma_start(out=out_rows[:, :, v0 : v0 + OUT_COLS], in_=y[:])
+            return yb
+
+        def out_planes(yb, v0):
+            cols = slice(v0, v0 + OUT_COLS)
+            nc.vector.quantize_mx(out=yq[:, cols].bitcast(FP8X4), scales=ys[:, cols], in_=yb[:])
+            nc.sync.dma_start(out=out_words[:, cols], in_=yq[:, cols].bitcast(I32))
+
+        pending = []
+        v0 = 0
+        for c, n in enumerate(CHUNKS):
+            zb = mix(c, v0, n)
+            for yb, w0 in pending:
+                out_planes(yb, w0)
+            zq, zs = quantize_z(c, zb, n)
+            pending = [(out_layer(zq, zs, z0, v0 + z0), v0 + z0) for z0 in range(0, n, OUT_COLS)]
+            v0 = v0 + n
+        for yb, w0 in pending:
+            out_planes(yb, w0)
+        for quad in range(4):
+            queue = nc.sync if quad % 2 == 0 else nc.scalar
+            queue.dma_start(
+                out=out_2[0, 4 * quad : 4 * quad + 4, :].bitcast(I32),
+                in_=ys[32 * quad : 32 * quad + 4, :].bitcast(I32),
+            )

@@ -20,7 +20,7 @@ P = 128
 PACK = 4
 GROUP = 16
 HALF = 512
-CHUNKS = (256, 128, 128)
+CHUNKS = (384, 128)
 OUT_COLS = 128
 
 
@@ -61,18 +61,19 @@ def tile_picked_tourney_none_po_kernel(
         xs_all = keep.tile([P, T], U8, name="xs_all", tag="slot_a", align_bytes=64)
         xw_all = keep.tile([P, T], I32, name="xw_all", align_bytes=64)
         w1_raw = keep.tile([P, 2 * H], U8, name="w1_raw", tag="slot_w", align_bytes=64)
-        w1s_raw = keep.tile([P, H], U8, name="w1s_raw", align_bytes=64)
+        w1s_raw = keep.tile([P, H], U8, name="w1s_raw", tag="slot_x", align_bytes=64)
         warm = keep.tile([P, 2], F32, name="warm")
 
-        nc.vector.memset(xs_all[:].bitcast(I32), 0)
+        nc.vector.memset(xs_all[:, : T // 2].bitcast(I32), 0)
+        nc.gpsimd.memset(xs_all[:, T // 2 :].bitcast(I32), 0)
         nc.vector.memset(w1s_raw[:].bitcast(I32), 0)
         nc.vector.memset(warm[:, 0:1], 0.0)
 
         nc.sync.dma_start(offs_sb[:], offs)
-        load_scale_rows(nc.scalar, xs_all, x_scales)
+        load_scale_rows(nc.sync, xs_all, x_scales)
         nc.sync.dma_start(right_sb[:], right)
         nc.sync.dma_start(left_sb[:], left)
-        nc.sync.dma_start(out=w1_raw[:].bitcast(I32), in_=w1_words[0].bitcast(I32))
+        nc.gpsimd.dma_start(out=w1_raw[:].bitcast(I32), in_=w1_words[0].bitcast(I32))
         nc.sync.dma_start(out=xw_all[:], in_=x_words[0].rearrange("p n t -> p (n t)").bitcast(I32))
         load_scale_rows(nc.scalar, w1s_raw, w1_scales)
         nc.scalar.activation(warm[:, 1:2], warm[:, 0:1], SIGMOID)
@@ -80,120 +81,118 @@ def tile_picked_tourney_none_po_kernel(
         xs = keep.tile([P, S], U8, name="xs", align_bytes=64)
         nc.vector.tensor_copy(xs[:], xs_all[:].indirect(offs_sb[:]))
         w1q = keep.tile([P, 2 * H], U8, name="w1q", tag="slot_b", align_bytes=64)
-        w1s = keep.tile([P, H], U8, name="w1s", align_bytes=64)
+        w1s = keep.tile([P, H], U8, name="w1s", tag="slot_s", align_bytes=64)
         w3q = keep.tile([P, 2 * N], U8, name="w3q", align_bytes=64)
-        w3s = keep.tile([P, N], U8, name="w3s", align_bytes=64)
         deal_fp4_words(nc, w1q, w1_raw)
-        w3_raw = keep.tile([P, 2 * N], U8, name="w3_raw", tag="slot_w", align_bytes=64)
+        deal_scale_bytes(nc, w1s, w1s_raw)
+        w3_pair = keep.tile([P, 3 * N], U8, name="w3_pair", tag="slot_w", align_bytes=64)
+        w3_raw, w3s_raw = w3_pair[:, : 2 * N], w3_pair[:, 2 * N :]
+        nc.gpsimd.memset(w3s_raw.bitcast(I32), 0)
         nc.sync.dma_start(out=w3_raw[:].bitcast(I32), in_=w3_words[0].bitcast(I32))
         w2_raw = keep.tile([P, PACK, H], F32, name="w2_raw", tag="slot_a", align_bytes=64)
         nc.sync.dma_start(out=w2_raw[:], in_=w2.rearrange("(p j) c -> p j c", j=PACK))
         xw = []
         for h in range(S // HALF):
-            xw_h = keep.tile([P, HALF], U32, name=f"xw{h}", align_bytes=64)
+            xw_h = keep.tile([P, HALF], U32, name=f"xw{h}", tag=("xw0", "slot_x")[h], align_bytes=64)
             nc.vector.tensor_copy(
                 xw_h[:], xw_all[:].bitcast(U32).indirect(offs_sb[:, h * HALF // GROUP : (h + 1) * HALF // GROUP])
             )
             xw.append(xw_h)
-            if h == 0:
-                deal_scale_bytes(nc, w1s, w1s_raw)
-        load_scale_rows(nc.sync, w1s_raw, w3_scales)
+        load_scale_rows(nc.sync, w3s_raw, w3_scales)
         deal_fp4_words(nc, w3q, w3_raw)
-        deal_scale_bytes(nc, w3s, w1s_raw)
 
-        def multiply(lhs, lhs_scale):
-            banks = []
-            for h in range(S // HALF):
-                cols = slice(h * HALF, (h + 1) * HALF)
-                acc = acc_pool.tile([P, HALF], F32, name="acc")
-                nc.tensor.matmul_mx(
-                    out=acc[:], lhsT=lhs, lhsT_scale=lhs_scale,
-                    rhs=xw[h][:].bitcast(FP8X4), rhs_scale=xs[:, cols], start=True, stop=True,
-                )
-                banks.append(acc)
-            return banks
+        def multiply(lhs, lhs_scale, h):
+            acc = acc_pool.tile([P, HALF], F32, name="acc")
+            nc.tensor.matmul_mx(
+                out=acc[:], lhsT=lhs, lhsT_scale=lhs_scale,
+                rhs=xw[h][:].bitcast(FP8X4), rhs_scale=xs[:, h * HALF : (h + 1) * HALF], start=True, stop=True,
+            )
+            return acc
 
-        def evacuate(name, banks):
-            rows = keep.tile([P, S], F32, name=name, align_bytes=64)
-            for h, acc in enumerate(banks):
-                nc.scalar.copy(rows[:, h * HALF : (h + 1) * HALF], acc[:])
-            return rows
+        def score_bank(t, h):
+            return multiply(w1q[:, 2 * P * t : 2 * P * (t + 1)].bitcast(FP4X4), w1s[:, P * t : P * (t + 1)], h)
 
-        s_acc = [
-            multiply(w1q[:, 2 * P * t : 2 * P * (t + 1)].bitcast(FP4X4), w1s[:, P * t : P * (t + 1)])
-            for t in range(3)
-        ]
-        s_rows = [evacuate(f"s{t}", s_acc[t]) for t in range(3)]
-        s_acc3 = multiply(w1q[:, 2 * P * 3 : 2 * P * 4].bitcast(FP4X4), w1s[:, P * 3 : P * 4])
+        s_rows = [keep.tile([P, S], F32, name=f"s{t}", align_bytes=64) for t in range(PACK)]
+        order = [(t, h) for pair in range(2) for h in range(2) for t in (2 * pair, 2 * pair + 1)]
+        s_banks = {th: score_bank(*th) for th in order[:6]}
+        for t, h in order[:3]:
+            nc.scalar.copy(s_rows[t][:, h * HALF : (h + 1) * HALF], s_banks[t, h][:])
+        nc.vector.tensor_copy(s_rows[1][:, HALF:], s_banks[1, 1][:])
+        for th in order[6:]:
+            s_banks[th] = score_bank(*th)
 
         w2b = keep.tile([P, H * PACK], BF16, name="w2b", tag="slot_b", align_bytes=64)
         w2b_v = w2b[:].rearrange("p (t m j) -> p m j t", t=PACK, j=PACK)
         w2_v = w2_raw[:].rearrange("p j (m t) -> p m j t", t=PACK)
         nc.scalar.copy(w2b_v, w2_v)
-        s_rows.append(evacuate("s3", s_acc3))
+        for t, h in order[4:]:
+            nc.scalar.copy(s_rows[t][:, h * HALF : (h + 1) * HALF], s_banks[t, h][:])
         w2q = keep.tile([P, H], U32, name="w2q", align_bytes=64)
         w2s = keep.tile([P, H], U8, name="w2s", align_bytes=64)
 
-        s_right = [keep.tile([P, V], F32, name=f"sr{t}") for t in range(3)]
+        s_right = [keep.tile([P, V], F32, name=f"sr{t}") for t in range(PACK)]
         diff = [keep.tile([P, V], F32, name=f"d{t}") for t in range(PACK)]
         q_all = keep.tile([P, 2 * PACK, V], F32, name="q_all", tag="slot_a", align_bytes=64)
         q_left = [q_all[:, 2 * t, :] for t in range(PACK)]
         q_right = [q_all[:, 2 * t + 1, :] for t in range(PACK)]
 
-        def fetch_right(t):
-            nc.vector.tensor_copy(s_right[t][:], s_rows[t][:].indirect(right_sb[:]))
+        def fetch_right(t, v0, n):
+            lst = right_sb[:, v0 // GROUP : (v0 + n) // GROUP]
+            nc.vector.tensor_copy(s_right[t][:, v0 : v0 + n], s_rows[t][:].indirect(lst))
 
-        def fetch_left(t):
-            nc.vector.tensor_tensor(diff[t][:], s_rows[t][:].indirect(left_sb[:]), s_right[t][:], ALU.subtract)
+        def fetch_left(t, v0, n):
+            lst = left_sb[:, v0 // GROUP : (v0 + n) // GROUP]
+            nc.vector.tensor_tensor(
+                diff[t][:, v0 : v0 + n], s_rows[t][:].indirect(lst), s_right[t][:, v0 : v0 + n], ALU.subtract
+            )
 
         def gates(t, cols):
             nc.scalar.activation(q_left[t][:, cols], diff[t][:, cols], SIGMOID)
             nc.scalar.activation(q_right[t][:, cols], diff[t][:, cols], SIGMOID, scale=-1.0)
 
-        fetch_right(0)
-        fetch_right(1)
-        fetch_left(0)
-        fetch_right(2)
-        fetch_left(1)
+        fetch_right(0, 0, V)
+        fetch_right(1, 0, V)
+        fetch_left(0, 0, V)
+        fetch_left(1, 0, V)
+        w3s = keep.tile([P, N], U8, name="w3s", tag="slot_s", align_bytes=64)
+        deal_scale_bytes(nc, w3s, w3s_raw)
         nc.vector.quantize_mx(out=w2q[:].bitcast(FP8X4), scales=w2s[:], in_=w2b[:])
-        s_right.append(keep.tile([P, V], F32, name="sr3", tag="slot_b", align_bytes=64))
-        fetch_right(3)
-        fetch_left(2)
-        fetch_left(3)
+        for t in (2, 3):
+            for fetch in (fetch_right, fetch_left):
+                for v0 in (0, V // 2):
+                    fetch(t, v0, V // 2)
 
-        val_rows = []
-        first, rest = slice(0, CHUNKS[0]), slice(CHUNKS[0], V)
+        val_rows = [keep.tile([P, S], F32, name=f"val{t}", align_bytes=64) for t in range(PACK)]
         gates(0, slice(0, V))
         gates(1, slice(0, V))
         for t in range(PACK):
-            banks = multiply(w2q[:, P * t : P * (t + 1)].bitcast(FP8X4), w2s[:, P * t : P * (t + 1)])
-            val_rows.append(evacuate(f"val{t}", banks))
+            for h in range(2):
+                acc = multiply(w2q[:, P * t : P * (t + 1)].bitcast(FP8X4), w2s[:, P * t : P * (t + 1)], h)
+                nc.scalar.copy(val_rows[t][:, h * HALF : (h + 1) * HALF], acc[:])
             if t >= 2:
-                gates(t, first)
-        gates(2, rest)
-        gates(3, rest)
+                gates(t, slice(0, V // 2))
+        gates(2, slice(V // 2, V))
+        gates(3, slice(V // 2, V))
 
         yq = keep.tile([P, V], U32, name="yq", align_bytes=64)
         ys = keep.tile([P, V], U8, name="ys", align_bytes=64)
         out_rows = out_0.rearrange("(p t) v -> p t v", t=PACK)
         out_words = out_1[0].rearrange("p n t -> p (n t)").bitcast(I32)
 
-        def mix(c, v0, n):
-            part_l = keep.tile([P, PACK, n], F32, name=f"pl{c}")
-            part_r = keep.tile([P, PACK, n], F32, name=f"pr{c}")
-            lst = slice(v0 // GROUP, (v0 + n) // GROUP)
-            for t in range(PACK):
-                nc.vector.tensor_tensor(
-                    part_l[:, t, :], val_rows[t][:].indirect(left_sb[:, lst]), q_left[t][:, v0 : v0 + n], ALU.mult
-                )
-                nc.vector.tensor_tensor(
-                    part_r[:, t, :], val_rows[t][:].indirect(right_sb[:, lst]), q_right[t][:, v0 : v0 + n], ALU.mult
-                )
-            zb = keep.tile([P, n * PACK], BF16, name=f"zb{c}", align_bytes=64)
+        def fetch_part(part, t, lists, gate, v0, n):
+            nc.vector.tensor_tensor(
+                part[:, t, :],
+                val_rows[t][:].indirect(lists[:, v0 // GROUP : (v0 + n) // GROUP]),
+                gate[t][:, v0 : v0 + n],
+                ALU.mult,
+            )
+
+        def add_parts(part_l, part_r, name, tag):
+            zb = keep.tile([P, OUT_COLS * PACK], BF16, name=name, tag=tag, align_bytes=64)
             nc.vector.tensor_tensor(
                 zb[:].rearrange("p (c i t) -> p c t i", i=4, t=PACK),
-                part_l[:].rearrange("p t (c i) -> p c t i", i=4),
-                part_r[:].rearrange("p t (c i) -> p c t i", i=4),
+                part_l.rearrange("p t (c i) -> p c t i", i=4),
+                part_r.rearrange("p t (c i) -> p c t i", i=4),
                 ALU.add,
             )
             return zb
@@ -201,7 +200,7 @@ def tile_picked_tourney_none_po_kernel(
         def quantize_z(c, zb, n):
             zq = keep.tile([P, n], U32, name=f"zq{c}", align_bytes=64)
             zs = keep.tile([P, n], U8, name=f"zs{c}", align_bytes=64)
-            nc.vector.quantize_mx(out=zq[:].bitcast(FP8X4), scales=zs[:], in_=zb[:])
+            nc.vector.quantize_mx(out=zq[:].bitcast(FP8X4), scales=zs[:], in_=zb)
             return zq, zs
 
         def out_layer(zq, zs, z0, v0):
@@ -215,27 +214,70 @@ def tile_picked_tourney_none_po_kernel(
                 )
             yb = keep.tile([P, OUT_COLS * PACK], BF16, name=f"yb{v0}", align_bytes=64)
             nc.scalar.copy(yb[:].rearrange("p (n t) -> p n t", t=PACK), acc[:].rearrange("p t n -> p n t"))
+            return acc, yb
+
+        def store_rows(acc, v0):
             y = keep.tile([P, PACK, OUT_COLS], F32, name=f"y{v0}")
             nc.scalar.copy(y[:], acc[:])
             nc.sync.dma_start(out=out_rows[:, :, v0 : v0 + OUT_COLS], in_=y[:])
-            return yb
 
         def out_planes(yb, v0):
             cols = slice(v0, v0 + OUT_COLS)
             nc.vector.quantize_mx(out=yq[:, cols].bitcast(FP8X4), scales=ys[:, cols], in_=yb[:])
             nc.sync.dma_start(out=out_words[:, cols], in_=yq[:, cols].bitcast(I32))
 
-        pending = []
-        v0 = 0
-        for c, n in enumerate(CHUNKS):
-            zb = mix(c, v0, n)
-            for yb, w0 in pending:
-                out_planes(yb, w0)
-            zq, zs = quantize_z(c, zb, n)
-            pending = [(out_layer(zq, zs, z0, v0 + z0), v0 + z0) for z0 in range(0, n, OUT_COLS)]
-            v0 = v0 + n
-        for yb, w0 in pending:
-            out_planes(yb, w0)
+        B = OUT_COLS
+        first_n, last_n = 3 * B, B
+        pl0 = keep.tile([P, PACK, 2 * B], F32, name="pl0")
+        pr0 = keep.tile([P, PACK, 2 * B], F32, name="pr0")
+        for t in range(PACK):
+            fetch_part(pl0, t, left_sb, q_left, 0, 2 * B)
+            fetch_part(pr0, t, right_sb, q_right, 0, 2 * B)
+        zb0 = add_parts(pl0[:, :, :B], pr0[:, :, :B], "zb0", "slot_z0")
+        zb1 = add_parts(pl0[:, :, B:], pr0[:, :, B:], "zb1", "slot_z1")
+        z0 = quantize_z(0, zb0[:], B)
+        z1 = quantize_z(1, zb1[:], B)
+        acc0, yb0 = out_layer(z0[0], z0[1], 0, 0)
+        store_rows(acc0, 0)
+        acc1, yb1 = out_layer(z1[0], z1[1], 0, B)
+        store_rows(acc1, B)
+        parts2 = keep.tile([P, 2 * PACK, B], F32, name="parts2", tag="slot_z0", align_bytes=64)
+        pl2, pr2 = parts2[:, :PACK, :], parts2[:, PACK:, :]
+        for t in range(PACK):
+            fetch_part(pl2, t, left_sb, q_left, 2 * B, B)
+            fetch_part(pr2, t, right_sb, q_right, 2 * B, B)
+        zb2 = add_parts(pl2, pr2, "zb2", "slot_z2")
+        z2 = quantize_z(2, zb2[:], B)
+        acc2, yb2 = out_layer(z2[0], z2[1], 0, 2 * B)
+        store_rows(acc2, 2 * B)
+        pr3 = keep.tile([P, PACK, B], F32, name="pr3", tag="slot_z1", align_bytes=64)
+        pl3 = keep.tile([P, PACK, B], F32, name="pl3", tag="slot_z2", align_bytes=64)
+        for t in range(PACK):
+            fetch_part(pr3, t, right_sb, q_right, 3 * B, B)
+        for t in range(PACK):
+            fetch_part(pl3, t, left_sb, q_left, 3 * B, B)
+        out_planes(yb0, 0)
+        zb3 = add_parts(pl3[:], pr3[:], "zb3", "zb3")
+        out_planes(yb1, B)
+        zq, zs = quantize_z(3, zb3[:], B)
+        y = keep.tile([P, PACK, last_n], F32, name="y_last")
+        for u in range(2):
+            acc = acc_pool.tile([P, 2, last_n], F32, name="ylast", tag="acc")
+            for e in range(2):
+                t = 2 * u + e
+                nc.tensor.matmul_mx(
+                    out=acc[:, e, :],
+                    lhsT=w3q[:, 2 * P * t : 2 * P * (t + 1)].bitcast(FP4X4), lhsT_scale=w3s[:, P * t : P * (t + 1)],
+                    rhs=zq[:].bitcast(FP8X4), rhs_scale=zs[:], start=True, stop=True,
+                )
+            nc.scalar.copy(y[:, 2 * u : 2 * u + 2, :], acc[:])
+        nc.sync.dma_start(out=out_rows[:, :, first_n:], in_=y[:])
+        out_planes(yb2, 2 * B)
+        yb = keep.tile([P, last_n * PACK], BF16, name="yb_last", align_bytes=64)
+        nc.vector.tensor_copy(
+            yb[:].rearrange("p (c i t) -> p c t i", i=4, t=PACK), y[:].rearrange("p t (c i) -> p c t i", i=4)
+        )
+        out_planes(yb, first_n)
         for quad in range(4):
             queue = nc.sync if quad % 2 == 0 else nc.scalar
             queue.dma_start(

@@ -125,8 +125,11 @@ def tile_picked_tourney_none_po_kernel(
         w2b_v = w2b[:].rearrange("p (t m j) -> p m j t", t=PACK, j=PACK)
         w2_v = w2_raw[:].rearrange("p j (m t) -> p m j t", t=PACK)
         nc.scalar.copy(w2b_v, w2_v)
-        for t, h in order[4:]:
-            nc.scalar.copy(s_rows[t][:, h * HALF : (h + 1) * HALF], s_banks[t, h][:])
+        for t, h in order[4:6]:
+            nc.scalar.copy(s_rows[t][:, :HALF], s_banks[t, h][:])
+        nc.scalar.copy(s_rows[3][:, HALF : S - 64], s_banks[3, 1][:, : HALF - 64])
+        nc.scalar.copy(s_rows[2][:, HALF:], s_banks[2, 1][:])
+        nc.scalar.copy(s_rows[3][:, S - 64 :], s_banks[3, 1][:, HALF - 64 :])
         w2q = keep.tile([P, H], U32, name="w2q", align_bytes=64)
         w2s = keep.tile([P, H], U8, name="w2s", align_bytes=64)
 
@@ -157,10 +160,10 @@ def tile_picked_tourney_none_po_kernel(
         w3s = keep.tile([P, N], U8, name="w3s", tag="slot_s", align_bytes=64)
         deal_scale_bytes(nc, w3s, w3s_raw)
         nc.vector.quantize_mx(out=w2q[:].bitcast(FP8X4), scales=w2s[:], in_=w2b[:])
-        for t in (2, 3):
-            for fetch in (fetch_right, fetch_left):
-                for v0 in (0, V // 2):
-                    fetch(t, v0, V // 2)
+        fetch_right(2, 0, V)
+        fetch_right(3, 0, V)
+        fetch_left(2, 0, V)
+        fetch_left(3, 0, V)
 
         val_rows = [keep.tile([P, S], F32, name=f"val{t}", align_bytes=64) for t in range(PACK)]
         gates(0, slice(0, V))

@@ -20,7 +20,8 @@ P = 128
 PACK = 4
 GROUP = 16
 HALF = 512
-CHUNKS = (384, 128)
+PIECE = 256
+LATE = 32
 OUT_COLS = 128
 
 
@@ -32,15 +33,15 @@ def load_scale_rows(queue, plane, scales):
         )
 
 
-def deal_fp4_words(nc, dealt, raw):
-    nc.vector.tensor_copy(
+def deal_fp4_words(engine, dealt, raw):
+    engine.tensor_copy(
         out=dealt[:].rearrange("p (t m b) -> p t m b", t=PACK, b=2),
         in_=raw[:].rearrange("p (m t b) -> p t m b", t=PACK, b=2),
     )
 
 
-def deal_scale_bytes(nc, dealt, raw):
-    nc.vector.tensor_copy(
+def deal_scale_bytes(engine, dealt, raw):
+    engine.tensor_copy(
         out=dealt[:].rearrange("p (t m) -> p t m", t=PACK),
         in_=raw[:].rearrange("p (m t) -> p t m", t=PACK),
     )
@@ -52,81 +53,96 @@ def tile_picked_tourney_none_po_kernel(
     nc = tc.nc
     with ExitStack() as ctx:
         keep = ctx.enter_context(tc.tile_pool(name="keep", bufs=1))
-        acc_pool = ctx.enter_context(tc.psum_pool(name="acc", bufs=6))
-        out_pool = ctx.enter_context(tc.psum_pool(name="outp", bufs=2))
+        acc_pool = ctx.enter_context(tc.psum_pool(name="acc", bufs=8))
 
         offs_sb = keep.tile([P, S // GROUP], U16, name="offs_sb")
         left_sb = keep.tile([P, V // GROUP], U16, name="left_sb")
         right_sb = keep.tile([P, V // GROUP], U16, name="right_sb")
-        xs_all = keep.tile([P, T], U8, name="xs_all", tag="slot_a", align_bytes=64)
+        xs_all = keep.tile([P, T], U8, name="xs_all", align_bytes=64)
         xw_all = keep.tile([P, T], I32, name="xw_all", align_bytes=64)
-        w1_raw = keep.tile([P, 2 * H], U8, name="w1_raw", tag="slot_w", align_bytes=64)
-        w1s_raw = keep.tile([P, H], U8, name="w1s_raw", tag="slot_x", align_bytes=64)
+        w1_raw = keep.tile([P, 2 * H], U8, name="w1_raw", align_bytes=64)
+        w1s_raw = keep.tile([P, H], U8, name="w1s_raw", align_bytes=64)
+        w3_raw = keep.tile([P, 2 * N], U8, name="w3_raw", align_bytes=64)
+        w3s_raw = keep.tile([P, N], U8, name="w3s_raw", align_bytes=64)
+        w2_raw = keep.tile([P, PACK, H], F32, name="w2_raw", align_bytes=64)
         warm = keep.tile([P, 2], F32, name="warm")
 
         nc.vector.memset(xs_all[:, : T // 2].bitcast(I32), 0)
         nc.gpsimd.memset(xs_all[:, T // 2 :].bitcast(I32), 0)
-        nc.vector.memset(w1s_raw[:].bitcast(I32), 0)
         nc.vector.memset(warm[:, 0:1], 0.0)
+        nc.vector.memset(w1s_raw[:].bitcast(I32), 0)
+        nc.vector.memset(w3s_raw[:].bitcast(I32), 0)
 
         nc.sync.dma_start(offs_sb[:], offs)
+        nc.scalar.dma_start(out=w1_raw[:].bitcast(I32), in_=w1_words[0].bitcast(I32))
         load_scale_rows(nc.sync, xs_all, x_scales)
+        nc.sync.dma_start(out=xw_all[:], in_=x_words[0].rearrange("p n t -> p (n t)").bitcast(I32))
+        load_scale_rows(nc.sync, w1s_raw, w1_scales)
+        nc.sync.dma_start(out=w3_raw[:].bitcast(I32), in_=w3_words[0].bitcast(I32))
+        nc.sync.dma_start(out=w2_raw[:], in_=w2.rearrange("(p j) c -> p j c", j=PACK))
         nc.sync.dma_start(right_sb[:], right)
         nc.sync.dma_start(left_sb[:], left)
-        nc.gpsimd.dma_start(out=w1_raw[:].bitcast(I32), in_=w1_words[0].bitcast(I32))
-        nc.sync.dma_start(out=xw_all[:], in_=x_words[0].rearrange("p n t -> p (n t)").bitcast(I32))
-        load_scale_rows(nc.scalar, w1s_raw, w1_scales)
+        load_scale_rows(nc.sync, w3s_raw, w3_scales)
         nc.scalar.activation(warm[:, 1:2], warm[:, 0:1], SIGMOID)
 
+        w1q = keep.tile([P, 2 * H], U8, name="w1q", align_bytes=64)
+        w1s = keep.tile([P, H], U8, name="w1s", align_bytes=64)
+        w3q = keep.tile([P, 2 * N], U8, name="w3q", align_bytes=64)
+        w3s = keep.tile([P, N], U8, name="w3s", align_bytes=64)
+        deal_fp4_words(nc.vector, w1q, w1_raw)
+        deal_scale_bytes(nc.gpsimd, w1s, w1s_raw)
+        deal_fp4_words(nc.gpsimd, w3q, w3_raw)
+        deal_scale_bytes(nc.gpsimd, w3s, w3s_raw)
         xs = keep.tile([P, S], U8, name="xs", align_bytes=64)
         nc.vector.tensor_copy(xs[:], xs_all[:].indirect(offs_sb[:]))
-        w1q = keep.tile([P, 2 * H], U8, name="w1q", tag="slot_b", align_bytes=64)
-        w1s = keep.tile([P, H], U8, name="w1s", tag="slot_s", align_bytes=64)
-        w3q = keep.tile([P, 2 * N], U8, name="w3q", align_bytes=64)
-        deal_fp4_words(nc, w1q, w1_raw)
-        deal_scale_bytes(nc, w1s, w1s_raw)
-        w3_pair = keep.tile([P, 3 * N], U8, name="w3_pair", tag="slot_w", align_bytes=64)
-        w3_raw, w3s_raw = w3_pair[:, : 2 * N], w3_pair[:, 2 * N :]
-        nc.gpsimd.memset(w3s_raw.bitcast(I32), 0)
-        nc.sync.dma_start(out=w3_raw[:].bitcast(I32), in_=w3_words[0].bitcast(I32))
-        w2_raw = keep.tile([P, PACK, H], F32, name="w2_raw", tag="slot_a", align_bytes=64)
-        nc.sync.dma_start(out=w2_raw[:], in_=w2.rearrange("(p j) c -> p j c", j=PACK))
-        xw = []
-        for h in range(S // HALF):
-            xw_h = keep.tile([P, HALF], U32, name=f"xw{h}", tag=("xw0", "slot_x")[h], align_bytes=64)
+        xw = keep.tile([P, S], U32, name="xw", align_bytes=64)
+        for j in range(S // PIECE):
             nc.vector.tensor_copy(
-                xw_h[:], xw_all[:].bitcast(U32).indirect(offs_sb[:, h * HALF // GROUP : (h + 1) * HALF // GROUP])
+                xw[:, j * PIECE : (j + 1) * PIECE],
+                xw_all[:].bitcast(U32).indirect(offs_sb[:, j * PIECE // GROUP : (j + 1) * PIECE // GROUP]),
             )
-            xw.append(xw_h)
-        load_scale_rows(nc.sync, w3s_raw, w3_scales)
-        deal_fp4_words(nc, w3q, w3_raw)
 
-        def multiply(lhs, lhs_scale, h):
-            acc = acc_pool.tile([P, HALF], F32, name="acc")
+        def multiply(acc, lhs, lhs_scale, cols):
             nc.tensor.matmul_mx(
-                out=acc[:], lhsT=lhs, lhsT_scale=lhs_scale,
-                rhs=xw[h][:].bitcast(FP8X4), rhs_scale=xs[:, h * HALF : (h + 1) * HALF], start=True, stop=True,
+                out=acc, lhsT=lhs, lhsT_scale=lhs_scale,
+                rhs=xw[:, cols].bitcast(FP8X4), rhs_scale=xs[:, cols], start=True, stop=True,
             )
-            return acc
 
-        def score_bank(t, h):
-            return multiply(w1q[:, 2 * P * t : 2 * P * (t + 1)].bitcast(FP4X4), w1s[:, P * t : P * (t + 1)], h)
+        def score(acc, t, cols):
+            multiply(acc, w1q[:, 2 * P * t : 2 * P * (t + 1)].bitcast(FP4X4), w1s[:, P * t : P * (t + 1)], cols)
 
         s_rows = [keep.tile([P, S], F32, name=f"s{t}", align_bytes=64) for t in range(PACK)]
-        order = [(t, h) for pair in range(2) for h in range(2) for t in (2 * pair, 2 * pair + 1)]
-        s_banks = {th: score_bank(*th) for th in order[:6]}
-        for t, h in order[:3]:
-            nc.scalar.copy(s_rows[t][:, h * HALF : (h + 1) * HALF], s_banks[t, h][:])
-        nc.vector.tensor_copy(s_rows[1][:, HALF:], s_banks[1, 1][:])
-        for th in order[6:]:
-            s_banks[th] = score_bank(*th)
+        last = S // PIECE - 1
+        for j in range(last):
+            cols = slice(j * PIECE, (j + 1) * PIECE)
+            acc = acc_pool.tile([P, 2, PIECE], F32, name="acc", tag="acc")
+            for t in range(2):
+                score(acc[:, t, :], t, cols)
+            nc.scalar.copy(s_rows[0][:, cols], acc[:, 0, :])
+            if j < last - 1:
+                nc.scalar.copy(s_rows[1][:, cols], acc[:, 1, :])
+            else:
+                nc.scalar.copy(s_rows[1][:, cols.start : cols.stop - LATE], acc[:, 1, : PIECE - LATE])
+                held, held_cols = acc, slice(cols.stop - LATE, cols.stop)
+        cols = slice(last * PIECE, S)
+        tail_banks = [acc_pool.tile([P, PIECE], F32, name=f"tail{t}", tag="acc") for t in range(2)]
+        for t in range(2):
+            score(tail_banks[t][:], t, cols)
+        nc.scalar.copy(s_rows[0][:, cols], tail_banks[0][:])
+        nc.scalar.copy(s_rows[1][:, held_cols], held[:, 1, PIECE - LATE :])
+        nc.vector.tensor_copy(s_rows[1][:, cols], tail_banks[1][:])
+        s_banks = {}
+        for h in range(2):
+            for t in (2, 3):
+                s_banks[t, h] = acc_pool.tile([P, HALF], F32, name=f"acc{t}{h}", tag="acc")
+                score(s_banks[t, h][:], t, slice(h * HALF, (h + 1) * HALF))
 
-        w2b = keep.tile([P, H * PACK], BF16, name="w2b", tag="slot_b", align_bytes=64)
+        w2b = keep.tile([P, H * PACK], BF16, name="w2b", align_bytes=64)
         w2b_v = w2b[:].rearrange("p (t m j) -> p m j t", t=PACK, j=PACK)
         w2_v = w2_raw[:].rearrange("p j (m t) -> p m j t", t=PACK)
         nc.scalar.copy(w2b_v, w2_v)
-        for t, h in order[4:6]:
-            nc.scalar.copy(s_rows[t][:, :HALF], s_banks[t, h][:])
+        for t in (2, 3):
+            nc.scalar.copy(s_rows[t][:, :HALF], s_banks[t, 0][:])
         nc.scalar.copy(s_rows[3][:, HALF : S - 64], s_banks[3, 1][:, : HALF - 64])
         nc.scalar.copy(s_rows[2][:, HALF:], s_banks[2, 1][:])
         nc.scalar.copy(s_rows[3][:, S - 64 :], s_banks[3, 1][:, HALF - 64 :])
@@ -135,7 +151,7 @@ def tile_picked_tourney_none_po_kernel(
 
         s_right = [keep.tile([P, V], F32, name=f"sr{t}") for t in range(PACK)]
         diff = [keep.tile([P, V], F32, name=f"d{t}") for t in range(PACK)]
-        q_all = keep.tile([P, 2 * PACK, V], F32, name="q_all", tag="slot_a", align_bytes=64)
+        q_all = keep.tile([P, 2 * PACK, V], F32, name="q_all", align_bytes=64)
         q_left = [q_all[:, 2 * t, :] for t in range(PACK)]
         q_right = [q_all[:, 2 * t + 1, :] for t in range(PACK)]
 
@@ -157,8 +173,6 @@ def tile_picked_tourney_none_po_kernel(
         fetch_right(1, 0, V)
         fetch_left(0, 0, V)
         fetch_left(1, 0, V)
-        w3s = keep.tile([P, N], U8, name="w3s", tag="slot_s", align_bytes=64)
-        deal_scale_bytes(nc, w3s, w3s_raw)
         nc.vector.quantize_mx(out=w2q[:].bitcast(FP8X4), scales=w2s[:], in_=w2b[:])
         fetch_right(2, 0, V)
         fetch_right(3, 0, V)
@@ -170,7 +184,11 @@ def tile_picked_tourney_none_po_kernel(
         gates(1, slice(0, V))
         for t in range(PACK):
             for h in range(2):
-                acc = multiply(w2q[:, P * t : P * (t + 1)].bitcast(FP8X4), w2s[:, P * t : P * (t + 1)], h)
+                acc = acc_pool.tile([P, HALF], F32, name="vacc", tag="acc")
+                multiply(
+                    acc[:], w2q[:, P * t : P * (t + 1)].bitcast(FP8X4), w2s[:, P * t : P * (t + 1)],
+                    slice(h * HALF, (h + 1) * HALF),
+                )
                 nc.scalar.copy(val_rows[t][:, h * HALF : (h + 1) * HALF], acc[:])
             if t >= 2:
                 gates(t, slice(0, V // 2))
@@ -207,7 +225,7 @@ def tile_picked_tourney_none_po_kernel(
             return zq, zs
 
         def out_layer(zq, zs, z0, v0):
-            acc = out_pool.tile([P, PACK, OUT_COLS], F32, name="yacc")
+            acc = acc_pool.tile([P, PACK, OUT_COLS], F32, name="yacc", tag="acc")
             for t in range(PACK):
                 nc.tensor.matmul_mx(
                     out=acc[:, t, :],

@@ -25,8 +25,8 @@ LATE = 32
 OUT_COLS = 128
 
 
-def load_scale_rows(queue, plane, scales):
-    for quad in range(4):
+def load_scale_rows(queues, plane, scales):
+    for quad, queue in enumerate(queues):
         queue.dma_start(
             out=plane[32 * quad : 32 * quad + 4, :].bitcast(I32),
             in_=scales[0, 4 * quad : 4 * quad + 4, :].bitcast(I32),
@@ -40,10 +40,10 @@ def deal_fp4_words(engine, dealt, raw):
     )
 
 
-def deal_scale_bytes(engine, dealt, raw):
+def deal_scale_bytes(engine, dealt, raw, tiles):
     engine.tensor_copy(
-        out=dealt[:].rearrange("p (t m) -> p t m", t=PACK),
-        in_=raw[:].rearrange("p (m t) -> p t m", t=PACK),
+        out=dealt[:].rearrange("p (t m) -> p t m", t=PACK)[:, tiles],
+        in_=raw[:].rearrange("p (m t) -> p t m", t=PACK)[:, tiles],
     )
 
 
@@ -75,14 +75,14 @@ def tile_picked_tourney_none_po_kernel(
 
         nc.sync.dma_start(offs_sb[:], offs)
         nc.scalar.dma_start(out=w1_raw[:].bitcast(I32), in_=w1_words[0].bitcast(I32))
-        load_scale_rows(nc.sync, xs_all, x_scales)
+        load_scale_rows([nc.sync] * 4, xs_all, x_scales)
         nc.sync.dma_start(out=xw_all[:], in_=x_words[0].rearrange("p n t -> p (n t)").bitcast(I32))
-        load_scale_rows(nc.sync, w1s_raw, w1_scales)
+        load_scale_rows([nc.sync] * 3 + [nc.gpsimd], w1s_raw, w1_scales)
         nc.sync.dma_start(out=w3_raw[:].bitcast(I32), in_=w3_words[0].bitcast(I32))
-        nc.sync.dma_start(out=w2_raw[:], in_=w2.rearrange("(p j) c -> p j c", j=PACK))
         nc.sync.dma_start(right_sb[:], right)
+        nc.sync.dma_start(out=w2_raw[:], in_=w2.rearrange("(p j) c -> p j c", j=PACK))
         nc.sync.dma_start(left_sb[:], left)
-        load_scale_rows(nc.sync, w3s_raw, w3_scales)
+        load_scale_rows([nc.sync] * 4, w3s_raw, w3_scales)
         nc.scalar.activation(warm[:, 1:2], warm[:, 0:1], SIGMOID)
 
         w1q = keep.tile([P, 2 * H], U8, name="w1q", align_bytes=64)
@@ -90,9 +90,10 @@ def tile_picked_tourney_none_po_kernel(
         w3q = keep.tile([P, 2 * N], U8, name="w3q", align_bytes=64)
         w3s = keep.tile([P, N], U8, name="w3s", align_bytes=64)
         deal_fp4_words(nc.vector, w1q, w1_raw)
-        deal_scale_bytes(nc.gpsimd, w1s, w1s_raw)
+        deal_scale_bytes(nc.gpsimd, w1s, w1s_raw, slice(0, 2))
+        deal_scale_bytes(nc.gpsimd, w1s, w1s_raw, slice(2, 4))
         deal_fp4_words(nc.gpsimd, w3q, w3_raw)
-        deal_scale_bytes(nc.gpsimd, w3s, w3s_raw)
+        deal_scale_bytes(nc.gpsimd, w3s, w3s_raw, slice(0, 4))
         xs = keep.tile([P, S], U8, name="xs", align_bytes=64)
         nc.vector.tensor_copy(xs[:], xs_all[:].indirect(offs_sb[:]))
         xw = keep.tile([P, S], U32, name="xw", align_bytes=64)
@@ -112,25 +113,24 @@ def tile_picked_tourney_none_po_kernel(
             multiply(acc, w1q[:, 2 * P * t : 2 * P * (t + 1)].bitcast(FP4X4), w1s[:, P * t : P * (t + 1)], cols)
 
         s_rows = [keep.tile([P, S], F32, name=f"s{t}", align_bytes=64) for t in range(PACK)]
-        last = S // PIECE - 1
-        for j in range(last):
+        shared = []
+        for j in range(2):
             cols = slice(j * PIECE, (j + 1) * PIECE)
             acc = acc_pool.tile([P, 2, PIECE], F32, name="acc", tag="acc")
             for t in range(2):
                 score(acc[:, t, :], t, cols)
-            nc.scalar.copy(s_rows[0][:, cols], acc[:, 0, :])
-            if j < last - 1:
-                nc.scalar.copy(s_rows[1][:, cols], acc[:, 1, :])
-            else:
-                nc.scalar.copy(s_rows[1][:, cols.start : cols.stop - LATE], acc[:, 1, : PIECE - LATE])
-                held, held_cols = acc, slice(cols.stop - LATE, cols.stop)
-        cols = slice(last * PIECE, S)
-        tail_banks = [acc_pool.tile([P, PIECE], F32, name=f"tail{t}", tag="acc") for t in range(2)]
-        for t in range(2):
-            score(tail_banks[t][:], t, cols)
-        nc.scalar.copy(s_rows[0][:, cols], tail_banks[0][:])
-        nc.scalar.copy(s_rows[1][:, held_cols], held[:, 1, PIECE - LATE :])
-        nc.vector.tensor_copy(s_rows[1][:, cols], tail_banks[1][:])
+            shared.append(acc)
+        nc.scalar.copy(s_rows[0][:, :PIECE], shared[0][:, 0, :])
+        nc.scalar.copy(s_rows[1][:, :PIECE], shared[0][:, 1, :])
+        nc.scalar.copy(s_rows[0][:, PIECE:HALF], shared[1][:, 0, :])
+        nc.scalar.copy(s_rows[1][:, PIECE : HALF - LATE], shared[1][:, 1, : PIECE - LATE])
+        for j in range(2, 4):
+            cols = slice(j * PIECE, (j + 1) * PIECE)
+            for t, copy in enumerate((nc.scalar.copy, nc.vector.tensor_copy)):
+                acc = acc_pool.tile([P, PIECE], F32, name="own", tag="acc")
+                score(acc[:], t, cols)
+                copy(s_rows[t][:, cols], acc[:])
+        nc.scalar.copy(s_rows[1][:, HALF - LATE : HALF], shared[1][:, 1, PIECE - LATE :])
         s_banks = {}
         for h in range(2):
             for t in (2, 3):

@@ -19,10 +19,11 @@ SIGMOID = mybir.ActivationFunctionType.Sigmoid
 P = 128
 PACK = 4
 GROUP = 16
-HALF = 512
+BANK = 512
 PIECE = 256
-LATE = 32
-OUT_COLS = 128
+BLOCK = 128
+LATE_FIRST = 32
+LATE_SECOND = 64
 
 
 def load_scale_rows(queues, plane, scales):
@@ -47,13 +48,25 @@ def deal_scale_bytes(engine, dealt, raw, tiles):
     )
 
 
+def block(c):
+    return slice(c * BLOCK, (c + 1) * BLOCK)
+
+
+def interleaved(tile):
+    return tile.rearrange("p (c i t) -> p c t i", i=4, t=PACK)
+
+
+def by_row_tile(tile):
+    return tile.rearrange("p t (c i) -> p c t i", i=4)
+
+
 def tile_picked_tourney_none_po_kernel(
     tc, x_words, x_scales, w1_words, w1_scales, w2, w3_words, w3_scales, offs, left, right, out_0, out_1, out_2
 ):
     nc = tc.nc
     with ExitStack() as ctx:
         keep = ctx.enter_context(tc.tile_pool(name="keep", bufs=1))
-        acc_pool = ctx.enter_context(tc.psum_pool(name="acc", bufs=8))
+        banks = ctx.enter_context(tc.psum_pool(name="banks", bufs=8))
 
         offs_sb = keep.tile([P, S // GROUP], U16, name="offs_sb")
         left_sb = keep.tile([P, V // GROUP], U16, name="left_sb")
@@ -91,9 +104,10 @@ def tile_picked_tourney_none_po_kernel(
         w3s = keep.tile([P, N], U8, name="w3s", align_bytes=64)
         deal_fp4_words(nc.vector, w1q, w1_raw)
         deal_scale_bytes(nc.gpsimd, w1s, w1s_raw, slice(0, 2))
-        deal_scale_bytes(nc.gpsimd, w1s, w1s_raw, slice(2, 4))
+        deal_scale_bytes(nc.gpsimd, w1s, w1s_raw, slice(2, PACK))
         deal_fp4_words(nc.gpsimd, w3q, w3_raw)
-        deal_scale_bytes(nc.gpsimd, w3s, w3s_raw, slice(0, 4))
+        deal_scale_bytes(nc.gpsimd, w3s, w3s_raw, slice(0, PACK))
+
         xs = keep.tile([P, S], U8, name="xs", align_bytes=64)
         nc.vector.tensor_copy(xs[:], xs_all[:].indirect(offs_sb[:]))
         xw = keep.tile([P, S], U32, name="xw", align_bytes=64)
@@ -103,49 +117,50 @@ def tile_picked_tourney_none_po_kernel(
                 xw_all[:].bitcast(U32).indirect(offs_sb[:, j * PIECE // GROUP : (j + 1) * PIECE // GROUP]),
             )
 
-        def multiply(acc, lhs, lhs_scale, cols):
+        def times_x(acc, lhs, lhs_scale, cols):
             nc.tensor.matmul_mx(
                 out=acc, lhsT=lhs, lhsT_scale=lhs_scale,
                 rhs=xw[:, cols].bitcast(FP8X4), rhs_scale=xs[:, cols], start=True, stop=True,
             )
 
         def score(acc, t, cols):
-            multiply(acc, w1q[:, 2 * P * t : 2 * P * (t + 1)].bitcast(FP4X4), w1s[:, P * t : P * (t + 1)], cols)
+            times_x(acc, w1q[:, 2 * P * t : 2 * P * (t + 1)].bitcast(FP4X4), w1s[:, P * t : P * (t + 1)], cols)
 
         s_rows = [keep.tile([P, S], F32, name=f"s{t}", align_bytes=64) for t in range(PACK)]
         shared = []
         for j in range(2):
-            cols = slice(j * PIECE, (j + 1) * PIECE)
-            acc = acc_pool.tile([P, 2, PIECE], F32, name="acc", tag="acc")
+            acc = banks.tile([P, 2, PIECE], F32, name="s_shared", tag="bank")
             for t in range(2):
-                score(acc[:, t, :], t, cols)
+                score(acc[:, t, :], t, slice(j * PIECE, (j + 1) * PIECE))
             shared.append(acc)
         nc.scalar.copy(s_rows[0][:, :PIECE], shared[0][:, 0, :])
         nc.scalar.copy(s_rows[1][:, :PIECE], shared[0][:, 1, :])
-        nc.scalar.copy(s_rows[0][:, PIECE:HALF], shared[1][:, 0, :])
-        nc.scalar.copy(s_rows[1][:, PIECE : HALF - LATE], shared[1][:, 1, : PIECE - LATE])
-        for j in range(2, 4):
+        nc.scalar.copy(s_rows[0][:, PIECE : 2 * PIECE], shared[1][:, 0, :])
+        nc.scalar.copy(s_rows[1][:, PIECE : 2 * PIECE - LATE_FIRST], shared[1][:, 1, : PIECE - LATE_FIRST])
+        for j in range(2, S // PIECE):
             cols = slice(j * PIECE, (j + 1) * PIECE)
             for t, copy in enumerate((nc.scalar.copy, nc.vector.tensor_copy)):
-                acc = acc_pool.tile([P, PIECE], F32, name="own", tag="acc")
+                acc = banks.tile([P, PIECE], F32, name="s_own", tag="bank")
                 score(acc[:], t, cols)
                 copy(s_rows[t][:, cols], acc[:])
-        nc.scalar.copy(s_rows[1][:, HALF - LATE : HALF], shared[1][:, 1, PIECE - LATE :])
+        nc.scalar.copy(s_rows[1][:, 2 * PIECE - LATE_FIRST : 2 * PIECE], shared[1][:, 1, PIECE - LATE_FIRST :])
+
         s_banks = {}
-        for h in range(2):
+        for h in range(S // BANK):
             for t in (2, 3):
-                s_banks[t, h] = acc_pool.tile([P, HALF], F32, name=f"acc{t}{h}", tag="acc")
-                score(s_banks[t, h][:], t, slice(h * HALF, (h + 1) * HALF))
+                s_banks[t, h] = banks.tile([P, BANK], F32, name=f"s_bank{t}{h}", tag="bank")
+                score(s_banks[t, h][:], t, slice(h * BANK, (h + 1) * BANK))
 
         w2b = keep.tile([P, H * PACK], BF16, name="w2b", align_bytes=64)
-        w2b_v = w2b[:].rearrange("p (t m j) -> p m j t", t=PACK, j=PACK)
-        w2_v = w2_raw[:].rearrange("p j (m t) -> p m j t", t=PACK)
-        nc.scalar.copy(w2b_v, w2_v)
+        nc.scalar.copy(
+            w2b[:].rearrange("p (t m j) -> p m j t", t=PACK, j=PACK),
+            w2_raw[:].rearrange("p j (m t) -> p m j t", t=PACK),
+        )
         for t in (2, 3):
-            nc.scalar.copy(s_rows[t][:, :HALF], s_banks[t, 0][:])
-        nc.scalar.copy(s_rows[3][:, HALF : S - 64], s_banks[3, 1][:, : HALF - 64])
-        nc.scalar.copy(s_rows[2][:, HALF:], s_banks[2, 1][:])
-        nc.scalar.copy(s_rows[3][:, S - 64 :], s_banks[3, 1][:, HALF - 64 :])
+            nc.scalar.copy(s_rows[t][:, :BANK], s_banks[t, 0][:])
+        nc.scalar.copy(s_rows[3][:, BANK : S - LATE_SECOND], s_banks[3, 1][:, : BANK - LATE_SECOND])
+        nc.scalar.copy(s_rows[2][:, BANK:], s_banks[2, 1][:])
+        nc.scalar.copy(s_rows[3][:, S - LATE_SECOND :], s_banks[3, 1][:, BANK - LATE_SECOND :])
         w2q = keep.tile([P, H], U32, name="w2q", align_bytes=64)
         w2s = keep.tile([P, H], U8, name="w2s", align_bytes=64)
 
@@ -155,150 +170,119 @@ def tile_picked_tourney_none_po_kernel(
         q_left = [q_all[:, 2 * t, :] for t in range(PACK)]
         q_right = [q_all[:, 2 * t + 1, :] for t in range(PACK)]
 
-        def fetch_right(t, v0, n):
-            lst = right_sb[:, v0 // GROUP : (v0 + n) // GROUP]
-            nc.vector.tensor_copy(s_right[t][:, v0 : v0 + n], s_rows[t][:].indirect(lst))
+        def score_differences(pair):
+            for t in pair:
+                nc.vector.tensor_copy(s_right[t][:], s_rows[t][:].indirect(right_sb[:]))
+            for t in pair:
+                nc.vector.tensor_tensor(diff[t][:], s_rows[t][:].indirect(left_sb[:]), s_right[t][:], ALU.subtract)
 
-        def fetch_left(t, v0, n):
-            lst = left_sb[:, v0 // GROUP : (v0 + n) // GROUP]
-            nc.vector.tensor_tensor(
-                diff[t][:, v0 : v0 + n], s_rows[t][:].indirect(lst), s_right[t][:, v0 : v0 + n], ALU.subtract
-            )
+        def gates(t, pairs_l, pairs_r):
+            nc.scalar.activation(q_left[t][:, pairs_l], diff[t][:, pairs_l], SIGMOID)
+            nc.scalar.activation(q_right[t][:, pairs_r], diff[t][:, pairs_r], SIGMOID, scale=-1.0)
 
-        def gates(t, cols):
-            nc.scalar.activation(q_left[t][:, cols], diff[t][:, cols], SIGMOID)
-            nc.scalar.activation(q_right[t][:, cols], diff[t][:, cols], SIGMOID, scale=-1.0)
-
-        fetch_right(0, 0, V)
-        fetch_right(1, 0, V)
-        fetch_left(0, 0, V)
-        fetch_left(1, 0, V)
+        score_differences((0, 1))
         nc.vector.quantize_mx(out=w2q[:].bitcast(FP8X4), scales=w2s[:], in_=w2b[:])
-        fetch_right(2, 0, V)
-        fetch_right(3, 0, V)
-        fetch_left(2, 0, V)
-        fetch_left(3, 0, V)
+        score_differences((2, 3))
 
         val_rows = [keep.tile([P, S], F32, name=f"val{t}", align_bytes=64) for t in range(PACK)]
-        gates(0, slice(0, V))
-        gates(1, slice(0, V))
+        blocks01, blocks23 = slice(0, 2 * BLOCK), slice(2 * BLOCK, V)
+        blocks012 = slice(0, 3 * BLOCK)
+        gates(0, blocks012, blocks01)
+        gates(1, blocks012, blocks01)
         for t in range(PACK):
-            for h in range(2):
-                acc = acc_pool.tile([P, HALF], F32, name="vacc", tag="acc")
-                multiply(
-                    acc[:], w2q[:, P * t : P * (t + 1)].bitcast(FP8X4), w2s[:, P * t : P * (t + 1)],
-                    slice(h * HALF, (h + 1) * HALF),
-                )
-                nc.scalar.copy(val_rows[t][:, h * HALF : (h + 1) * HALF], acc[:])
+            for h in range(S // BANK):
+                cols = slice(h * BANK, (h + 1) * BANK)
+                acc = banks.tile([P, BANK], F32, name="val_bank", tag="bank")
+                times_x(acc[:], w2q[:, P * t : P * (t + 1)].bitcast(FP8X4), w2s[:, P * t : P * (t + 1)], cols)
+                nc.scalar.copy(val_rows[t][:, cols], acc[:])
             if t >= 2:
-                gates(t, slice(0, V // 2))
-        gates(2, slice(V // 2, V))
-        gates(3, slice(V // 2, V))
+                gates(t, blocks012, blocks01)
+        for t in range(PACK):
+            gates(t, block(3), blocks23)
 
         yq = keep.tile([P, V], U32, name="yq", align_bytes=64)
         ys = keep.tile([P, V], U8, name="ys", align_bytes=64)
         out_rows = out_0.rearrange("(p t) v -> p t v", t=PACK)
         out_words = out_1[0].rearrange("p n t -> p (n t)").bitcast(I32)
 
-        def fetch_part(part, t, lists, gate, v0, n):
+        def gated_values(part, t, lists, gate, pairs):
             nc.vector.tensor_tensor(
                 part[:, t, :],
-                val_rows[t][:].indirect(lists[:, v0 // GROUP : (v0 + n) // GROUP]),
-                gate[t][:, v0 : v0 + n],
+                val_rows[t][:].indirect(lists[:, pairs.start // GROUP : pairs.stop // GROUP]),
+                gate[t][:, pairs],
                 ALU.mult,
             )
 
-        def add_parts(part_l, part_r, name, tag):
-            zb = keep.tile([P, OUT_COLS * PACK], BF16, name=name, tag=tag, align_bytes=64)
-            nc.vector.tensor_tensor(
-                zb[:].rearrange("p (c i t) -> p c t i", i=4, t=PACK),
-                part_l.rearrange("p t (c i) -> p c t i", i=4),
-                part_r.rearrange("p t (c i) -> p c t i", i=4),
-                ALU.add,
-            )
+        def add_parts(part_l, part_r, c):
+            zb = keep.tile([P, BLOCK * PACK], BF16, name=f"zb{c}", tag=f"zb{c}", align_bytes=64)
+            nc.vector.tensor_tensor(interleaved(zb[:]), by_row_tile(part_l), by_row_tile(part_r), ALU.add)
             return zb
 
-        def quantize_z(c, zb, n):
-            zq = keep.tile([P, n], U32, name=f"zq{c}", align_bytes=64)
-            zs = keep.tile([P, n], U8, name=f"zs{c}", align_bytes=64)
-            nc.vector.quantize_mx(out=zq[:].bitcast(FP8X4), scales=zs[:], in_=zb)
+        def quantize_z(zb, c):
+            zq = keep.tile([P, BLOCK], U32, name=f"zq{c}", align_bytes=64)
+            zs = keep.tile([P, BLOCK], U8, name=f"zs{c}", align_bytes=64)
+            nc.vector.quantize_mx(out=zq[:].bitcast(FP8X4), scales=zs[:], in_=zb[:])
             return zq, zs
 
-        def out_layer(zq, zs, z0, v0):
-            acc = acc_pool.tile([P, PACK, OUT_COLS], F32, name="yacc", tag="acc")
+        def times_w3(acc, t, z):
+            nc.tensor.matmul_mx(
+                out=acc,
+                lhsT=w3q[:, 2 * P * t : 2 * P * (t + 1)].bitcast(FP4X4), lhsT_scale=w3s[:, P * t : P * (t + 1)],
+                rhs=z[0][:].bitcast(FP8X4), rhs_scale=z[1][:], start=True, stop=True,
+            )
+
+        def last_layer(z, c):
+            acc = banks.tile([P, PACK, BLOCK], F32, name="y_bank", tag="bank")
             for t in range(PACK):
-                nc.tensor.matmul_mx(
-                    out=acc[:, t, :],
-                    lhsT=w3q[:, 2 * P * t : 2 * P * (t + 1)].bitcast(FP4X4), lhsT_scale=w3s[:, P * t : P * (t + 1)],
-                    rhs=zq[:, z0 : z0 + OUT_COLS].bitcast(FP8X4), rhs_scale=zs[:, z0 : z0 + OUT_COLS],
-                    start=True, stop=True,
-                )
-            yb = keep.tile([P, OUT_COLS * PACK], BF16, name=f"yb{v0}", align_bytes=64)
+                times_w3(acc[:, t, :], t, z)
+            yb = keep.tile([P, BLOCK * PACK], BF16, name=f"yb{c}", align_bytes=64)
             nc.scalar.copy(yb[:].rearrange("p (n t) -> p n t", t=PACK), acc[:].rearrange("p t n -> p n t"))
-            return acc, yb
-
-        def store_rows(acc, v0):
-            y = keep.tile([P, PACK, OUT_COLS], F32, name=f"y{v0}")
+            y = keep.tile([P, PACK, BLOCK], F32, name=f"y{c}")
             nc.scalar.copy(y[:], acc[:])
-            nc.sync.dma_start(out=out_rows[:, :, v0 : v0 + OUT_COLS], in_=y[:])
+            nc.sync.dma_start(out=out_rows[:, :, block(c)], in_=y[:])
+            return yb
 
-        def out_planes(yb, v0):
-            cols = slice(v0, v0 + OUT_COLS)
-            nc.vector.quantize_mx(out=yq[:, cols].bitcast(FP8X4), scales=ys[:, cols], in_=yb[:])
-            nc.sync.dma_start(out=out_words[:, cols], in_=yq[:, cols].bitcast(I32))
+        def quantize_y(yb, c):
+            nc.vector.quantize_mx(out=yq[:, block(c)].bitcast(FP8X4), scales=ys[:, block(c)], in_=yb[:])
 
-        B = OUT_COLS
-        first_n, last_n = 3 * B, B
-        pl0 = keep.tile([P, PACK, 2 * B], F32, name="pl0")
-        pr0 = keep.tile([P, PACK, 2 * B], F32, name="pr0")
+        left012 = keep.tile([P, PACK, 3 * BLOCK], F32, name="left012", tag="left012", align_bytes=64)
+        right01 = keep.tile([P, PACK, 2 * BLOCK], F32, name="right01")
         for t in range(PACK):
-            fetch_part(pl0, t, left_sb, q_left, 0, 2 * B)
-            fetch_part(pr0, t, right_sb, q_right, 0, 2 * B)
-        zb0 = add_parts(pl0[:, :, :B], pr0[:, :, :B], "zb0", "slot_z0")
-        zb1 = add_parts(pl0[:, :, B:], pr0[:, :, B:], "zb1", "slot_z1")
-        z0 = quantize_z(0, zb0[:], B)
-        z1 = quantize_z(1, zb1[:], B)
-        acc0, yb0 = out_layer(z0[0], z0[1], 0, 0)
-        store_rows(acc0, 0)
-        acc1, yb1 = out_layer(z1[0], z1[1], 0, B)
-        store_rows(acc1, B)
-        parts2 = keep.tile([P, 2 * PACK, B], F32, name="parts2", tag="slot_z0", align_bytes=64)
-        pl2, pr2 = parts2[:, :PACK, :], parts2[:, PACK:, :]
+            gated_values(left012, t, left_sb, q_left, blocks012)
+            gated_values(right01, t, right_sb, q_right, blocks01)
+        zb01 = [add_parts(left012[:, :, block(c)], right01[:, :, block(c)], c) for c in range(2)]
+        z01 = [quantize_z(zb01[c], c) for c in range(2)]
+        yb0, yb1 = [last_layer(z01[c], c) for c in range(2)]
+
+        right2 = keep.tile([P, PACK, BLOCK], F32, name="right2")
         for t in range(PACK):
-            fetch_part(pl2, t, left_sb, q_left, 2 * B, B)
-            fetch_part(pr2, t, right_sb, q_right, 2 * B, B)
-        zb2 = add_parts(pl2, pr2, "zb2", "slot_z2")
-        z2 = quantize_z(2, zb2[:], B)
-        acc2, yb2 = out_layer(z2[0], z2[1], 0, 2 * B)
-        store_rows(acc2, 2 * B)
-        pr3 = keep.tile([P, PACK, B], F32, name="pr3", tag="slot_z1", align_bytes=64)
-        pl3 = keep.tile([P, PACK, B], F32, name="pl3", tag="slot_z2", align_bytes=64)
+            gated_values(right2, t, right_sb, q_right, block(2))
+        yb2 = last_layer(quantize_z(add_parts(left012[:, :, block(2)], right2[:], 2), 2), 2)
+        right3 = keep.tile([P, PACK, BLOCK], F32, name="right3", tag="zb1", align_bytes=64)
+        left3 = keep.tile([P, PACK, BLOCK], F32, name="left3", tag="left012", align_bytes=64)
         for t in range(PACK):
-            fetch_part(pr3, t, right_sb, q_right, 3 * B, B)
+            gated_values(right3, t, right_sb, q_right, block(3))
         for t in range(PACK):
-            fetch_part(pl3, t, left_sb, q_left, 3 * B, B)
-        out_planes(yb0, 0)
-        zb3 = add_parts(pl3[:], pr3[:], "zb3", "zb3")
-        out_planes(yb1, B)
-        zq, zs = quantize_z(3, zb3[:], B)
-        y = keep.tile([P, PACK, last_n], F32, name="y_last")
+            gated_values(left3, t, left_sb, q_left, block(3))
+
+        quantize_y(yb0, 0)
+        zb3 = add_parts(left3[:], right3[:], 3)
+        quantize_y(yb1, 1)
+        nc.sync.dma_start(out=out_words[:, blocks01], in_=yq[:, blocks01].bitcast(I32))
+        z3 = quantize_z(zb3, 3)
+
+        y3 = keep.tile([P, PACK, BLOCK], F32, name="y3")
         for u in range(2):
-            acc = acc_pool.tile([P, 2, last_n], F32, name="ylast", tag="acc")
+            acc = banks.tile([P, 2, BLOCK], F32, name="y3_bank", tag="bank")
             for e in range(2):
-                t = 2 * u + e
-                nc.tensor.matmul_mx(
-                    out=acc[:, e, :],
-                    lhsT=w3q[:, 2 * P * t : 2 * P * (t + 1)].bitcast(FP4X4), lhsT_scale=w3s[:, P * t : P * (t + 1)],
-                    rhs=zq[:].bitcast(FP8X4), rhs_scale=zs[:], start=True, stop=True,
-                )
-            nc.scalar.copy(y[:, 2 * u : 2 * u + 2, :], acc[:])
-        nc.sync.dma_start(out=out_rows[:, :, first_n:], in_=y[:])
-        out_planes(yb2, 2 * B)
-        yb = keep.tile([P, last_n * PACK], BF16, name="yb_last", align_bytes=64)
-        nc.vector.tensor_copy(
-            yb[:].rearrange("p (c i t) -> p c t i", i=4, t=PACK), y[:].rearrange("p t (c i) -> p c t i", i=4)
-        )
-        out_planes(yb, first_n)
+                times_w3(acc[:, e, :], 2 * u + e, z3)
+            nc.scalar.copy(y3[:, 2 * u : 2 * u + 2, :], acc[:])
+        nc.sync.dma_start(out=out_rows[:, :, block(3)], in_=y3[:])
+        quantize_y(yb2, 2)
+        yb3 = keep.tile([P, BLOCK * PACK], BF16, name="yb3", align_bytes=64)
+        nc.vector.tensor_copy(interleaved(yb3[:]), by_row_tile(y3[:]))
+        quantize_y(yb3, 3)
+        nc.sync.dma_start(out=out_words[:, blocks23], in_=yq[:, blocks23].bitcast(I32))
         for quad in range(4):
             queue = nc.sync if quad % 2 == 0 else nc.scalar
             queue.dma_start(

@@ -1,6 +1,7 @@
 from contextlib import ExitStack
 
 import concourse.mybir as mybir
+from concourse.masks import make_identity
 
 K, T, S, V, N, H = 512, 2048, 1024, 512, 512, 512
 FLOPS = 2 * K * H * S * 2 + 2 * H * N * V
@@ -76,7 +77,7 @@ def tile_picked_tourney_none_po_kernel(
         w1_raw = keep.tile([P, 2 * H], U8, name="w1_raw", align_bytes=64)
         w1s_raw = keep.tile([P, H], U8, name="w1s_raw", align_bytes=64)
         w3_raw = keep.tile([P, 2 * N], U8, name="w3_raw", align_bytes=64)
-        w3s_raw = keep.tile([P, N], U8, name="w3s_raw", align_bytes=64)
+        w3s_raw = keep.tile([P, N], U8, name="w3s_raw", tag="w3s_raw", align_bytes=64)
         w2_raw = keep.tile([P, PACK, H], F32, name="w2_raw", align_bytes=64)
         warm = keep.tile([P, 2], F32, name="warm")
 
@@ -107,6 +108,9 @@ def tile_picked_tourney_none_po_kernel(
         deal_scale_bytes(nc.gpsimd, w1s, w1s_raw, slice(2, PACK))
         deal_fp4_words(nc.gpsimd, w3q, w3_raw)
         deal_scale_bytes(nc.gpsimd, w3s, w3s_raw, slice(0, PACK))
+
+        ident = keep.tile([P, P], F32, name="ident", tag="w3s_raw", align_bytes=64)
+        make_identity(nc, ident[:])
 
         xs = keep.tile([P, S], U8, name="xs", align_bytes=64)
         nc.vector.tensor_copy(xs[:], xs_all[:].indirect(offs_sb[:]))
@@ -165,20 +169,22 @@ def tile_picked_tourney_none_po_kernel(
         w2s = keep.tile([P, H], U8, name="w2s", align_bytes=64)
 
         s_right = [keep.tile([P, V], F32, name=f"sr{t}") for t in range(PACK)]
-        diff = [keep.tile([P, V], F32, name=f"d{t}") for t in range(PACK)]
-        q_all = keep.tile([P, 2 * PACK, V], F32, name="q_all", align_bytes=64)
-        q_left = [q_all[:, 2 * t, :] for t in range(PACK)]
-        q_right = [q_all[:, 2 * t + 1, :] for t in range(PACK)]
+        diff = keep.tile([P, PACK, V], F32, name="diff", align_bytes=64)
+        q_left = keep.tile([P, PACK, V], F32, name="q_left", align_bytes=64)
+        q_right = keep.tile([P, PACK, V], F32, name="q_right", align_bytes=64)
 
         def score_differences(pair):
             for t in pair:
                 nc.vector.tensor_copy(s_right[t][:], s_rows[t][:].indirect(right_sb[:]))
             for t in pair:
-                nc.vector.tensor_tensor(diff[t][:], s_rows[t][:].indirect(left_sb[:]), s_right[t][:], ALU.subtract)
+                nc.vector.tensor_tensor(diff[:, t, :], s_rows[t][:].indirect(left_sb[:]), s_right[t][:], ALU.subtract)
 
-        def gates(t, pairs_l, pairs_r):
-            nc.scalar.activation(q_left[t][:, pairs_l], diff[t][:, pairs_l], SIGMOID)
-            nc.scalar.activation(q_right[t][:, pairs_r], diff[t][:, pairs_r], SIGMOID, scale=-1.0)
+        def gate(out, tiles, pairs, sign):
+            nc.scalar.activation(out, diff[:, tiles, pairs], SIGMOID, scale=sign)
+
+        def gates(t, pairs):
+            gate(q_left[:, t, pairs], t, pairs, 1.0)
+            gate(q_right[:, t, pairs], t, pairs, -1.0)
 
         score_differences((0, 1))
         nc.vector.quantize_mx(out=w2q[:].bitcast(FP8X4), scales=w2s[:], in_=w2b[:])
@@ -186,9 +192,8 @@ def tile_picked_tourney_none_po_kernel(
 
         val_rows = [keep.tile([P, S], F32, name=f"val{t}", align_bytes=64) for t in range(PACK)]
         blocks01, blocks23 = slice(0, 2 * BLOCK), slice(2 * BLOCK, V)
-        blocks012 = slice(0, 3 * BLOCK)
-        gates(0, blocks012, blocks01)
-        gates(1, blocks012, blocks01)
+        gates(0, blocks01)
+        gates(1, blocks01)
         for t in range(PACK):
             for h in range(S // BANK):
                 cols = slice(h * BANK, (h + 1) * BANK)
@@ -196,20 +201,20 @@ def tile_picked_tourney_none_po_kernel(
                 times_x(acc[:], w2q[:, P * t : P * (t + 1)].bitcast(FP8X4), w2s[:, P * t : P * (t + 1)], cols)
                 nc.scalar.copy(val_rows[t][:, cols], acc[:])
             if t >= 2:
-                gates(t, blocks012, blocks01)
-        for t in range(PACK):
-            gates(t, block(3), blocks23)
+                gates(t, blocks01)
+        gate(q_right[:, :, blocks23], slice(0, PACK), blocks23, -1.0)
+        gate(q_left[:, :3, block(2)], slice(0, 3), block(2), 1.0)
 
         yq = keep.tile([P, V], U32, name="yq", align_bytes=64)
         ys = keep.tile([P, V], U8, name="ys", align_bytes=64)
         out_rows = out_0.rearrange("(p t) v -> p t v", t=PACK)
         out_words = out_1[0].rearrange("p n t -> p (n t)").bitcast(I32)
 
-        def gated_values(part, t, lists, gate, pairs):
+        def gated_values(part, t, lists, weight, pairs):
             nc.vector.tensor_tensor(
                 part[:, t, :],
                 val_rows[t][:].indirect(lists[:, pairs.start // GROUP : pairs.stop // GROUP]),
-                gate[t][:, pairs],
+                weight,
                 ALU.mult,
             )
 
@@ -221,7 +226,7 @@ def tile_picked_tourney_none_po_kernel(
         def quantize_z(zb, c):
             zq = keep.tile([P, BLOCK], U32, name=f"zq{c}", align_bytes=64)
             zs = keep.tile([P, BLOCK], U8, name=f"zs{c}", align_bytes=64)
-            nc.vector.quantize_mx(out=zq[:].bitcast(FP8X4), scales=zs[:], in_=zb[:])
+            nc.vector.quantize_mx(out=zq[:].bitcast(FP8X4), scales=zs[:], in_=zb)
             return zq, zs
 
         def times_w3(acc, t, z):
@@ -245,31 +250,58 @@ def tile_picked_tourney_none_po_kernel(
         def quantize_y(yb, c):
             nc.vector.quantize_mx(out=yq[:, block(c)].bitcast(FP8X4), scales=ys[:, block(c)], in_=yb[:])
 
-        left012 = keep.tile([P, PACK, 3 * BLOCK], F32, name="left012", tag="left012", align_bytes=64)
+        left01 = keep.tile([P, PACK, 2 * BLOCK], F32, name="left01")
         right01 = keep.tile([P, PACK, 2 * BLOCK], F32, name="right01")
+        back = [banks.tile([P, 2, BLOCK], F32, name=f"back{c}", tag="bank") for c in range(2)]
+        for u in range(2):
+            sums = banks.tile([P, 2, 2, P], F32, name=f"sums{u}", tag="bank")
+            for e in range(2):
+                t = 2 * u + e
+                gated_values(left01, t, left_sb, q_left[:, t, blocks01], blocks01)
+                gated_values(right01, t, right_sb, q_right[:, t, blocks01], blocks01)
+                for c in range(2):
+                    for part, first in ((left01, True), (right01, False)):
+                        nc.tensor.matmul(
+                            sums[:, c, e, :], lhsT=part[:, t, block(c)], rhs=ident[:],
+                            start=first, stop=not first, is_transpose=True,
+                        )
+            turned = keep.tile([P, 2, P, 2], BF16, name=f"turned{u}", tag=f"turned{u}", align_bytes=64)
+            for c in range(2):
+                nc.scalar.copy(turned[:, c], sums[:, c].rearrange("v e p -> v p e"))
+                nc.tensor.transpose(
+                    back[c][:, u, :], turned[:, c].rearrange("v p e -> v (p e)").bitcast(F32), ident[:]
+                )
+        zb01 = keep.tile([P, 2, BLOCK * PACK], BF16, name="zb01", align_bytes=64)
+        for c in range(2):
+            nc.scalar.copy(
+                zb01[:, c, :].bitcast(F32).rearrange("p (v u) -> p v u", u=2), back[c][:].rearrange("p u v -> p v u")
+            )
+        z01 = [quantize_z(zb01[:, c, :], c) for c in range(2)]
+        q_late = keep.tile([P, PACK + 1, BLOCK], F32, name="q_late", tag="turned1", align_bytes=64)
+        gate(q_late[:, PACK, :], 3, block(2), 1.0)
         for t in range(PACK):
-            gated_values(left012, t, left_sb, q_left, blocks012)
-            gated_values(right01, t, right_sb, q_right, blocks01)
-        zb01 = [add_parts(left012[:, :, block(c)], right01[:, :, block(c)], c) for c in range(2)]
-        z01 = [quantize_z(zb01[c], c) for c in range(2)]
+            gate(q_late[:, t, :], t, block(3), 1.0)
         yb0, yb1 = [last_layer(z01[c], c) for c in range(2)]
 
-        right2 = keep.tile([P, PACK, BLOCK], F32, name="right2")
+        right2 = keep.tile([P, PACK, BLOCK], F32, name="right2", tag="right2", align_bytes=64)
+        left2 = keep.tile([P, PACK, BLOCK], F32, name="left2")
         for t in range(PACK):
-            gated_values(right2, t, right_sb, q_right, block(2))
-        yb2 = last_layer(quantize_z(add_parts(left012[:, :, block(2)], right2[:], 2), 2), 2)
-        right3 = keep.tile([P, PACK, BLOCK], F32, name="right3", tag="zb1", align_bytes=64)
-        left3 = keep.tile([P, PACK, BLOCK], F32, name="left3", tag="left012", align_bytes=64)
+            gated_values(right2, t, right_sb, q_right[:, t, block(2)], block(2))
         for t in range(PACK):
-            gated_values(right3, t, right_sb, q_right, block(3))
+            gated_values(left2, t, left_sb, q_left[:, t, block(2)] if t < 3 else q_late[:, PACK, :], block(2))
+        yb2 = last_layer(quantize_z(add_parts(left2[:], right2[:], 2)[:], 2), 2)
+        left3 = keep.tile([P, PACK, BLOCK], F32, name="left3")
+        right3 = keep.tile([P, PACK, BLOCK], F32, name="right3", tag="right2", align_bytes=64)
         for t in range(PACK):
-            gated_values(left3, t, left_sb, q_left, block(3))
+            gated_values(left3, t, left_sb, q_late[:, t, :], block(3))
+        for t in range(PACK):
+            gated_values(right3, t, right_sb, q_right[:, t, block(3)], block(3))
 
         quantize_y(yb0, 0)
         zb3 = add_parts(left3[:], right3[:], 3)
         quantize_y(yb1, 1)
         nc.sync.dma_start(out=out_words[:, blocks01], in_=yq[:, blocks01].bitcast(I32))
-        z3 = quantize_z(zb3, 3)
+        z3 = quantize_z(zb3[:], 3)
 
         y3 = keep.tile([P, PACK, BLOCK], F32, name="y3")
         for u in range(2):

@@ -203,7 +203,8 @@ def tile_picked_tourney_none_po_kernel(
             if t >= 2:
                 gates(t, blocks01)
         gate(q_right[:, :, blocks23], slice(0, PACK), blocks23, -1.0)
-        gate(q_left[:, :3, block(2)], slice(0, 3), block(2), 1.0)
+        gate(q_left[:, :2, blocks23], slice(0, 2), blocks23, 1.0)
+        gate(q_left[:, 2:, block(2)], slice(2, PACK), block(2), 1.0)
 
         yq = keep.tile([P, V], U32, name="yq", align_bytes=64)
         ys = keep.tile([P, V], U8, name="ys", align_bytes=64)
@@ -219,7 +220,7 @@ def tile_picked_tourney_none_po_kernel(
             )
 
         def add_parts(part_l, part_r, c):
-            zb = keep.tile([P, BLOCK * PACK], BF16, name=f"zb{c}", tag=f"zb{c}", align_bytes=64)
+            zb = keep.tile([P, BLOCK * PACK], BF16, name=f"zb{c}", tag=f"zb{2 * c - 4}", align_bytes=64)
             nc.vector.tensor_tensor(interleaved(zb[:]), by_row_tile(part_l), by_row_tile(part_r), ALU.add)
             return zb
 
@@ -271,34 +272,33 @@ def tile_picked_tourney_none_po_kernel(
                 nc.tensor.transpose(
                     back[c][:, u, :], turned[:, c].rearrange("v p e -> v (p e)").bitcast(F32), ident[:]
                 )
-        zb01 = keep.tile([P, 2, BLOCK * PACK], BF16, name="zb01", align_bytes=64)
+        zb01 = [keep.tile([P, BLOCK * PACK], BF16, name=f"zb{c}", tag=f"zb{c}", align_bytes=64) for c in range(2)]
         for c in range(2):
             nc.scalar.copy(
-                zb01[:, c, :].bitcast(F32).rearrange("p (v u) -> p v u", u=2), back[c][:].rearrange("p u v -> p v u")
+                zb01[c][:].bitcast(F32).rearrange("p (v u) -> p v u", u=2), back[c][:].rearrange("p u v -> p v u")
             )
-        z01 = [quantize_z(zb01[:, c, :], c) for c in range(2)]
-        q_late = keep.tile([P, PACK + 1, BLOCK], F32, name="q_late", tag="turned1", align_bytes=64)
-        gate(q_late[:, PACK, :], 3, block(2), 1.0)
-        for t in range(PACK):
-            gate(q_late[:, t, :], t, block(3), 1.0)
+        z01 = [quantize_z(zb01[c][:], c) for c in range(2)]
+        q_late = keep.tile([P, 2, BLOCK], F32, name="q_late", tag="turned1", align_bytes=64)
+        gate(q_late[:], slice(2, PACK), block(3), 1.0)
         yb0, yb1 = [last_layer(z01[c], c) for c in range(2)]
 
         right2 = keep.tile([P, PACK, BLOCK], F32, name="right2", tag="right2", align_bytes=64)
-        left2 = keep.tile([P, PACK, BLOCK], F32, name="left2")
+        left23 = keep.tile([P, PACK, 2 * BLOCK], F32, name="left23")
         for t in range(PACK):
             gated_values(right2, t, right_sb, q_right[:, t, block(2)], block(2))
-        for t in range(PACK):
-            gated_values(left2, t, left_sb, q_left[:, t, block(2)] if t < 3 else q_late[:, PACK, :], block(2))
-        yb2 = last_layer(quantize_z(add_parts(left2[:], right2[:], 2)[:], 2), 2)
-        left3 = keep.tile([P, PACK, BLOCK], F32, name="left3")
+        for t in range(2):
+            gated_values(left23, t, left_sb, q_left[:, t, blocks23], blocks23)
+        for t in range(2, PACK):
+            gated_values(left23[:, :, block(0)], t, left_sb, q_left[:, t, block(2)], block(2))
+        yb2 = last_layer(quantize_z(add_parts(left23[:, :, block(0)], right2[:], 2)[:], 2), 2)
         right3 = keep.tile([P, PACK, BLOCK], F32, name="right3", tag="right2", align_bytes=64)
-        for t in range(PACK):
-            gated_values(left3, t, left_sb, q_late[:, t, :], block(3))
+        for t in range(2, PACK):
+            gated_values(left23[:, :, block(1)], t, left_sb, q_late[:, t - 2, :], block(3))
         for t in range(PACK):
             gated_values(right3, t, right_sb, q_right[:, t, block(3)], block(3))
 
         quantize_y(yb0, 0)
-        zb3 = add_parts(left3[:], right3[:], 3)
+        zb3 = add_parts(left23[:, :, block(1)], right3[:], 3)
         quantize_y(yb1, 1)
         nc.sync.dma_start(out=out_words[:, blocks01], in_=yq[:, blocks01].bitcast(I32))
         z3 = quantize_z(zb3[:], 3)

@@ -237,16 +237,27 @@ def tile_picked_tourney_none_po_kernel(
                 rhs=z[0][:].bitcast(FP8X4), rhs_scale=z[1][:], start=True, stop=True,
             )
 
-        def last_layer(z, c):
+        def last_layer(z):
             acc = banks.tile([P, PACK, BLOCK], F32, name="y_bank", tag="bank")
             for t in range(PACK):
                 times_w3(acc[:, t, :], t, z)
+            return acc
+
+        def round_from_bank(acc, c):
             yb = keep.tile([P, BLOCK * PACK], BF16, name=f"yb{c}", align_bytes=64)
             nc.scalar.copy(yb[:].rearrange("p (n t) -> p n t", t=PACK), acc[:].rearrange("p t n -> p n t"))
+            return yb
+
+        def round_from_rows(y, c):
+            yb = keep.tile([P, BLOCK * PACK], BF16, name=f"yb{c}", align_bytes=64)
+            nc.vector.tensor_copy(interleaved(yb[:]), by_row_tile(y[:]))
+            return yb
+
+        def store_rows(acc, c):
             y = keep.tile([P, PACK, BLOCK], F32, name=f"y{c}")
             nc.scalar.copy(y[:], acc[:])
             nc.sync.dma_start(out=out_rows[:, :, block(c)], in_=y[:])
-            return yb
+            return y
 
         def quantize_y(yb, c):
             nc.vector.quantize_mx(out=yq[:, block(c)].bitcast(FP8X4), scales=ys[:, block(c)], in_=yb[:])
@@ -280,7 +291,11 @@ def tile_picked_tourney_none_po_kernel(
         z01 = [quantize_z(zb01[c][:], c) for c in range(2)]
         q_late = keep.tile([P, 2, BLOCK], F32, name="q_late", tag="turned1", align_bytes=64)
         gate(q_late[:], slice(2, PACK), block(3), 1.0)
-        yb0, yb1 = [last_layer(z01[c], c) for c in range(2)]
+        yb01 = []
+        for c in range(2):
+            acc = last_layer(z01[c])
+            yb01.append(round_from_bank(acc, c))
+            store_rows(acc, c)
 
         right2 = keep.tile([P, PACK, BLOCK], F32, name="right2", tag="right2", align_bytes=64)
         left23 = keep.tile([P, PACK, 2 * BLOCK], F32, name="left23")
@@ -290,16 +305,16 @@ def tile_picked_tourney_none_po_kernel(
             gated_values(left23, t, left_sb, q_left[:, t, blocks23], blocks23)
         for t in range(2, PACK):
             gated_values(left23[:, :, block(0)], t, left_sb, q_left[:, t, block(2)], block(2))
-        yb2 = last_layer(quantize_z(add_parts(left23[:, :, block(0)], right2[:], 2)[:], 2), 2)
+        y2 = store_rows(last_layer(quantize_z(add_parts(left23[:, :, block(0)], right2[:], 2)[:], 2)), 2)
         right3 = keep.tile([P, PACK, BLOCK], F32, name="right3", tag="right2", align_bytes=64)
         for t in range(2, PACK):
             gated_values(left23[:, :, block(1)], t, left_sb, q_late[:, t - 2, :], block(3))
         for t in range(PACK):
             gated_values(right3, t, right_sb, q_right[:, t, block(3)], block(3))
 
-        quantize_y(yb0, 0)
+        quantize_y(yb01[0], 0)
         zb3 = add_parts(left23[:, :, block(1)], right3[:], 3)
-        quantize_y(yb1, 1)
+        quantize_y(yb01[1], 1)
         nc.sync.dma_start(out=out_words[:, blocks01], in_=yq[:, blocks01].bitcast(I32))
         z3 = quantize_z(zb3[:], 3)
 
@@ -310,10 +325,8 @@ def tile_picked_tourney_none_po_kernel(
                 times_w3(acc[:, e, :], 2 * u + e, z3)
             nc.scalar.copy(y3[:, 2 * u : 2 * u + 2, :], acc[:])
         nc.sync.dma_start(out=out_rows[:, :, block(3)], in_=y3[:])
-        quantize_y(yb2, 2)
-        yb3 = keep.tile([P, BLOCK * PACK], BF16, name="yb3", align_bytes=64)
-        nc.vector.tensor_copy(interleaved(yb3[:]), by_row_tile(y3[:]))
-        quantize_y(yb3, 3)
+        quantize_y(round_from_rows(y2, 2), 2)
+        quantize_y(round_from_rows(y3, 3), 3)
         nc.sync.dma_start(out=out_words[:, blocks23], in_=yq[:, blocks23].bitcast(I32))
         for quad in range(4):
             queue = nc.sync if quad % 2 == 0 else nc.scalar

@@ -1,7 +1,6 @@
 from contextlib import ExitStack
 
 import concourse.mybir as mybir
-from concourse.masks import make_identity
 
 K, T, S, V, N, H = 512, 2048, 1024, 512, 512, 512
 FLOPS = 2 * K * H * S * 2 + 2 * H * N * V
@@ -16,6 +15,7 @@ FP8X4 = mybir.dt.float8_e4m3fn_x4
 FP4X4 = mybir.dt.float4_e2m1fn_x4
 ALU = mybir.AluOpType
 SIGMOID = mybir.ActivationFunctionType.Sigmoid
+COPY = mybir.ActivationFunctionType.Copy
 
 P = 128
 PACK = 4
@@ -23,8 +23,6 @@ GROUP = 16
 BANK = 512
 PIECE = 256
 BLOCK = 128
-LATE_FIRST = 32
-LATE_SECOND = 64
 
 
 def load_scale_rows(queues, plane, scales):
@@ -78,7 +76,7 @@ def tile_picked_tourney_none_po_kernel(
         w1s_raw = keep.tile([P, H], U8, name="w1s_raw", align_bytes=64)
         w3_raw = keep.tile([P, 2 * N], U8, name="w3_raw", align_bytes=64)
         w3s_raw = keep.tile([P, N], U8, name="w3s_raw", tag="w3s_raw", align_bytes=64)
-        w2_raw = keep.tile([P, PACK, H], F32, name="w2_raw", align_bytes=64)
+        w2_raw = keep.tile([P, PACK, H], F32, name="w2_raw", tag="w2_raw", align_bytes=64)
         warm = keep.tile([P, 2], F32, name="warm")
 
         nc.vector.memset(xs_all[:, : T // 2].bitcast(I32), 0)
@@ -109,9 +107,6 @@ def tile_picked_tourney_none_po_kernel(
         deal_fp4_words(nc.gpsimd, w3q, w3_raw)
         deal_scale_bytes(nc.gpsimd, w3s, w3s_raw, slice(0, PACK))
 
-        ident = keep.tile([P, P], F32, name="ident", tag="w3s_raw", align_bytes=64)
-        make_identity(nc, ident[:])
-
         xs = keep.tile([P, S], U8, name="xs", align_bytes=64)
         nc.vector.tensor_copy(xs[:], xs_all[:].indirect(offs_sb[:]))
         xw = keep.tile([P, S], U32, name="xw", align_bytes=64)
@@ -131,103 +126,100 @@ def tile_picked_tourney_none_po_kernel(
             times_x(acc, w1q[:, 2 * P * t : 2 * P * (t + 1)].bitcast(FP4X4), w1s[:, P * t : P * (t + 1)], cols)
 
         s_rows = [keep.tile([P, S], F32, name=f"s{t}", align_bytes=64) for t in range(PACK)]
-        shared = []
-        for j in range(2):
+        for j in range(S // PIECE - 1):
+            cols = slice(j * PIECE, (j + 1) * PIECE)
             acc = banks.tile([P, 2, PIECE], F32, name="s_shared", tag="bank")
             for t in range(2):
-                score(acc[:, t, :], t, slice(j * PIECE, (j + 1) * PIECE))
-            shared.append(acc)
-        nc.scalar.copy(s_rows[0][:, :PIECE], shared[0][:, 0, :])
-        nc.scalar.copy(s_rows[1][:, :PIECE], shared[0][:, 1, :])
-        nc.scalar.copy(s_rows[0][:, PIECE : 2 * PIECE], shared[1][:, 0, :])
-        nc.scalar.copy(s_rows[1][:, PIECE : 2 * PIECE - LATE_FIRST], shared[1][:, 1, : PIECE - LATE_FIRST])
-        for j in range(2, S // PIECE):
-            cols = slice(j * PIECE, (j + 1) * PIECE)
-            for t, copy in enumerate((nc.scalar.copy, nc.vector.tensor_copy)):
-                acc = banks.tile([P, PIECE], F32, name="s_own", tag="bank")
-                score(acc[:], t, cols)
-                copy(s_rows[t][:, cols], acc[:])
-        nc.scalar.copy(s_rows[1][:, 2 * PIECE - LATE_FIRST : 2 * PIECE], shared[1][:, 1, PIECE - LATE_FIRST :])
+                score(acc[:, t, :], t, cols)
+            for t in range(2):
+                nc.scalar.copy(s_rows[t][:, cols], acc[:, t, :])
+        for t in range(2):
+            acc = banks.tile([P, PIECE], F32, name="s_own", tag="bank")
+            score(acc[:], t, slice(S - PIECE, S))
+            nc.scalar.copy(s_rows[t][:, S - PIECE :], acc[:])
 
         s_banks = {}
-        for h in range(S // BANK):
-            for t in (2, 3):
+        for t in (2, 3):
+            for h in range(S // BANK):
                 s_banks[t, h] = banks.tile([P, BANK], F32, name=f"s_bank{t}{h}", tag="bank")
                 score(s_banks[t, h][:], t, slice(h * BANK, (h + 1) * BANK))
 
-        w2b = keep.tile([P, H * PACK], BF16, name="w2b", align_bytes=64)
-        nc.scalar.copy(
+        w2b = keep.tile([P, H * PACK], BF16, name="w2b", tag="w2b", align_bytes=64)
+        nc.vector.tensor_copy(
             w2b[:].rearrange("p (t m j) -> p m j t", t=PACK, j=PACK),
             w2_raw[:].rearrange("p j (m t) -> p m j t", t=PACK),
         )
-        for t in (2, 3):
-            nc.scalar.copy(s_rows[t][:, :BANK], s_banks[t, 0][:])
-        nc.scalar.copy(s_rows[3][:, BANK : S - LATE_SECOND], s_banks[3, 1][:, : BANK - LATE_SECOND])
-        nc.scalar.copy(s_rows[2][:, BANK:], s_banks[2, 1][:])
-        nc.scalar.copy(s_rows[3][:, S - LATE_SECOND :], s_banks[3, 1][:, BANK - LATE_SECOND :])
         w2q = keep.tile([P, H], U32, name="w2q", align_bytes=64)
         w2s = keep.tile([P, H], U8, name="w2s", align_bytes=64)
 
-        s_right = [keep.tile([P, V], F32, name=f"sr{t}") for t in range(PACK)]
-        diff = keep.tile([P, PACK, V], F32, name="diff", align_bytes=64)
-        q_left = keep.tile([P, PACK, V], F32, name="q_left", align_bytes=64)
-        q_right = keep.tile([P, PACK, V], F32, name="q_right", align_bytes=64)
-
-        def score_differences(pair):
-            for t in pair:
-                nc.vector.tensor_copy(s_right[t][:], s_rows[t][:].indirect(right_sb[:]))
-            for t in pair:
-                nc.vector.tensor_tensor(diff[:, t, :], s_rows[t][:].indirect(left_sb[:]), s_right[t][:], ALU.subtract)
-
-        def gate(out, tiles, pairs, sign):
-            nc.scalar.activation(out, diff[:, tiles, pairs], SIGMOID, scale=sign)
-
-        def gates(t, pairs):
-            gate(q_left[:, t, pairs], t, pairs, 1.0)
-            gate(q_right[:, t, pairs], t, pairs, -1.0)
-
-        score_differences((0, 1))
-        nc.vector.quantize_mx(out=w2q[:].bitcast(FP8X4), scales=w2s[:], in_=w2b[:])
-        score_differences((2, 3))
-
+        sr01 = keep.tile([P, 2, V], F32, name="sr01", tag="w2_raw", align_bytes=64)
+        sr23 = keep.tile([P, 2, V], F32, name="sr23", align_bytes=64)
+        s_right = [sr01[:, 0, :], sr01[:, 1, :], sr23[:, 0, :], sr23[:, 1, :]]
         val_rows = [keep.tile([P, S], F32, name=f"val{t}", align_bytes=64) for t in range(PACK)]
-        blocks01, blocks23 = slice(0, 2 * BLOCK), slice(2 * BLOCK, V)
-        gates(0, blocks01)
-        gates(1, blocks01)
-        for t in range(PACK):
+        diff = keep.tile([P, PACK, V], F32, name="diff", tag="w2b", align_bytes=64)
+        q = keep.tile([P, PACK, V], F32, name="q", align_bytes=64)
+        val_right = keep.tile([P, PACK, V], F32, name="val_right", align_bytes=64)
+        part_left = keep.tile([P, PACK, V], F32, name="part_left", align_bytes=64)
+        part_right = keep.tile([P, PACK, V], F32, name="part_right", align_bytes=64)
+        first, second = slice(0, 2 * BLOCK), slice(2 * BLOCK, V)
+
+        def entries(lists, pairs):
+            return lists[:, pairs.start // GROUP : pairs.stop // GROUP]
+
+        def copy_scores(t):
+            for h in range(S // BANK):
+                nc.scalar.copy(s_rows[t][:, h * BANK : (h + 1) * BANK], s_banks[t, h][:])
+
+        def right_scores_vector(t):
+            nc.vector.tensor_copy(s_right[t], s_rows[t][:].indirect(right_sb[:]))
+
+        def right_scores_scalar(t):
+            nc.scalar.activation(s_right[t], s_rows[t][:].indirect(right_sb[:]), COPY)
+
+        def difference(t):
+            nc.vector.tensor_tensor(diff[:, t, :], s_rows[t][:].indirect(left_sb[:]), s_right[t], ALU.subtract)
+
+        def values(t, copy):
             for h in range(S // BANK):
                 cols = slice(h * BANK, (h + 1) * BANK)
                 acc = banks.tile([P, BANK], F32, name="val_bank", tag="bank")
                 times_x(acc[:], w2q[:, P * t : P * (t + 1)].bitcast(FP8X4), w2s[:, P * t : P * (t + 1)], cols)
-                nc.scalar.copy(val_rows[t][:, cols], acc[:])
-            if t >= 2:
-                gates(t, blocks01)
-        gate(q_right[:, :, blocks23], slice(0, PACK), blocks23, -1.0)
-        gate(q_left[:, :2, blocks23], slice(0, 2), blocks23, 1.0)
-        gate(q_left[:, 2:, block(2)], slice(2, PACK), block(2), 1.0)
+                copy(val_rows[t][:, cols], acc[:])
+
+        def gate(tiles, pairs):
+            nc.scalar.activation(q[:, tiles, pairs], diff[:, tiles, pairs], SIGMOID)
+
+        def right_values(t, pairs):
+            nc.scalar.activation(val_right[:, t, pairs], val_rows[t][:].indirect(entries(right_sb, pairs)), COPY)
+
+        def left_part(t, pairs):
+            nc.vector.tensor_tensor(
+                part_left[:, t, pairs], val_rows[t][:].indirect(entries(left_sb, pairs)), q[:, t, pairs], ALU.mult
+            )
+
+        def right_part(tiles, pairs):
+            nc.vector.scalar_tensor_tensor(
+                part_right[:, tiles, pairs], q[:, tiles, pairs], 1.0, val_right[:, tiles, pairs],
+                ALU.subtract, ALU.mult,
+            )
 
         yq = keep.tile([P, V], U32, name="yq", align_bytes=64)
         ys = keep.tile([P, V], U8, name="ys", align_bytes=64)
         out_rows = out_0.rearrange("(p t) v -> p t v", t=PACK)
         out_words = out_1[0].rearrange("p n t -> p (n t)").bitcast(I32)
 
-        def gated_values(part, t, lists, weight, pairs):
+        def mix(c):
+            zb = keep.tile([P, BLOCK * PACK], BF16, name=f"zb{c}", align_bytes=64)
             nc.vector.tensor_tensor(
-                part[:, t, :],
-                val_rows[t][:].indirect(lists[:, pairs.start // GROUP : pairs.stop // GROUP]),
-                weight,
-                ALU.mult,
+                interleaved(zb[:]), by_row_tile(part_left[:, :, block(c)]), by_row_tile(part_right[:, :, block(c)]),
+                ALU.subtract,
             )
-
-        def add_parts(part_l, part_r, c):
-            zb = keep.tile([P, BLOCK * PACK], BF16, name=f"zb{c}", tag=f"zb{2 * c - 4}", align_bytes=64)
-            nc.vector.tensor_tensor(interleaved(zb[:]), by_row_tile(part_l), by_row_tile(part_r), ALU.add)
             return zb
 
         def quantize_z(zb, c):
             zq = keep.tile([P, BLOCK], U32, name=f"zq{c}", align_bytes=64)
             zs = keep.tile([P, BLOCK], U8, name=f"zs{c}", align_bytes=64)
-            nc.vector.quantize_mx(out=zq[:].bitcast(FP8X4), scales=zs[:], in_=zb)
+            nc.vector.quantize_mx(out=zq[:].bitcast(FP8X4), scales=zs[:], in_=zb[:])
             return zq, zs
 
         def times_w3(acc, t, z):
@@ -262,61 +254,56 @@ def tile_picked_tourney_none_po_kernel(
         def quantize_y(yb, c):
             nc.vector.quantize_mx(out=yq[:, block(c)].bitcast(FP8X4), scales=ys[:, block(c)], in_=yb[:])
 
-        left01 = keep.tile([P, PACK, 2 * BLOCK], F32, name="left01")
-        right01 = keep.tile([P, PACK, 2 * BLOCK], F32, name="right01")
-        back = [banks.tile([P, 2, BLOCK], F32, name=f"back{c}", tag="bank") for c in range(2)]
-        for u in range(2):
-            sums = banks.tile([P, 2, 2, P], F32, name=f"sums{u}", tag="bank")
-            for e in range(2):
-                t = 2 * u + e
-                gated_values(left01, t, left_sb, q_left[:, t, blocks01], blocks01)
-                gated_values(right01, t, right_sb, q_right[:, t, blocks01], blocks01)
-                for c in range(2):
-                    for part, first in ((left01, True), (right01, False)):
-                        nc.tensor.matmul(
-                            sums[:, c, e, :], lhsT=part[:, t, block(c)], rhs=ident[:],
-                            start=first, stop=not first, is_transpose=True,
-                        )
-            turned = keep.tile([P, 2, P, 2], BF16, name=f"turned{u}", tag=f"turned{u}", align_bytes=64)
-            for c in range(2):
-                nc.scalar.copy(turned[:, c], sums[:, c].rearrange("v e p -> v p e"))
-                nc.tensor.transpose(
-                    back[c][:, u, :], turned[:, c].rearrange("v p e -> v (p e)").bitcast(F32), ident[:]
-                )
-        zb01 = [keep.tile([P, BLOCK * PACK], BF16, name=f"zb{c}", tag=f"zb{c}", align_bytes=64) for c in range(2)]
-        for c in range(2):
-            nc.scalar.copy(
-                zb01[c][:].bitcast(F32).rearrange("p (v u) -> p v u", u=2), back[c][:].rearrange("p u v -> p v u")
-            )
-        z01 = [quantize_z(zb01[c][:], c) for c in range(2)]
-        q_late = keep.tile([P, 2, BLOCK], F32, name="q_late", tag="turned1", align_bytes=64)
-        gate(q_late[:], slice(2, PACK), block(3), 1.0)
+        right_scores_vector(0)
+        nc.vector.quantize_mx(out=w2q[:].bitcast(FP8X4), scales=w2s[:], in_=w2b[:])
+        right_scores_vector(1)
+        copy_scores(2)
+        copy_scores(3)
+        difference(0)
+        right_scores_scalar(2)
+        difference(1)
+        values(0, nc.scalar.copy)
+        right_scores_scalar(3)
+        difference(2)
+        values(1, nc.scalar.copy)
+        difference(3)
+        gate(slice(0, 2), first)
+        values(2, nc.scalar.copy)
+        left_part(0, first)
+        left_part(1, first)
+        gate(slice(2, PACK), first)
+        values(3, nc.vector.tensor_copy)
+        for t in range(PACK):
+            right_values(t, first)
+        left_part(2, first)
+        left_part(3, first)
+        right_part(slice(0, 2), first)
+        right_part(slice(2, PACK), first)
+        gate(slice(0, PACK), second)
+        zb01 = [mix(c) for c in range(2)]
+        z01 = [quantize_z(zb01[c], c) for c in range(2)]
+        for t in range(PACK):
+            right_values(t, second)
+        left_part(0, second)
+        left_part(1, second)
+        left_part(2, block(2))
+        left_part(3, block(2))
         yb01 = []
         for c in range(2):
             acc = last_layer(z01[c])
             yb01.append(round_from_bank(acc, c))
             store_rows(acc, c)
-
-        right2 = keep.tile([P, PACK, BLOCK], F32, name="right2", tag="right2", align_bytes=64)
-        left23 = keep.tile([P, PACK, 2 * BLOCK], F32, name="left23")
-        for t in range(PACK):
-            gated_values(right2, t, right_sb, q_right[:, t, block(2)], block(2))
-        for t in range(2):
-            gated_values(left23, t, left_sb, q_left[:, t, blocks23], blocks23)
-        for t in range(2, PACK):
-            gated_values(left23[:, :, block(0)], t, left_sb, q_left[:, t, block(2)], block(2))
-        y2 = store_rows(last_layer(quantize_z(add_parts(left23[:, :, block(0)], right2[:], 2)[:], 2)), 2)
-        right3 = keep.tile([P, PACK, BLOCK], F32, name="right3", tag="right2", align_bytes=64)
-        for t in range(2, PACK):
-            gated_values(left23[:, :, block(1)], t, left_sb, q_late[:, t - 2, :], block(3))
-        for t in range(PACK):
-            gated_values(right3, t, right_sb, q_right[:, t, block(3)], block(3))
-
+        right_part(slice(0, 2), second)
+        right_part(slice(2, PACK), second)
+        zb2 = mix(2)
+        left_part(2, block(3))
+        y2 = store_rows(last_layer(quantize_z(zb2, 2)), 2)
+        left_part(3, block(3))
         quantize_y(yb01[0], 0)
-        zb3 = add_parts(left23[:, :, block(1)], right3[:], 3)
+        zb3 = mix(3)
         quantize_y(yb01[1], 1)
-        nc.sync.dma_start(out=out_words[:, blocks01], in_=yq[:, blocks01].bitcast(I32))
-        z3 = quantize_z(zb3[:], 3)
+        nc.sync.dma_start(out=out_words[:, first], in_=yq[:, first].bitcast(I32))
+        z3 = quantize_z(zb3, 3)
 
         y3 = keep.tile([P, PACK, BLOCK], F32, name="y3")
         for u in range(2):
@@ -327,7 +314,7 @@ def tile_picked_tourney_none_po_kernel(
         nc.sync.dma_start(out=out_rows[:, :, block(3)], in_=y3[:])
         quantize_y(round_from_rows(y2, 2), 2)
         quantize_y(round_from_rows(y3, 3), 3)
-        nc.sync.dma_start(out=out_words[:, blocks23], in_=yq[:, blocks23].bitcast(I32))
+        nc.sync.dma_start(out=out_words[:, second], in_=yq[:, second].bitcast(I32))
         for quad in range(4):
             queue = nc.sync if quad % 2 == 0 else nc.scalar
             queue.dma_start(

@@ -22,6 +22,7 @@ PACK = 4
 GROUP = 16
 BANK = 512
 PIECE = 256
+HALF = 256
 BLOCK = 128
 
 
@@ -100,12 +101,10 @@ def tile_picked_tourney_none_po_kernel(
         w1q = keep.tile([P, 2 * H], U8, name="w1q", align_bytes=64)
         w1s = keep.tile([P, H], U8, name="w1s", align_bytes=64)
         w3q = keep.tile([P, 2 * N], U8, name="w3q", align_bytes=64)
-        w3s = keep.tile([P, N], U8, name="w3s", align_bytes=64)
         deal_fp4_words(nc.vector, w1q, w1_raw)
         deal_scale_bytes(nc.gpsimd, w1s, w1s_raw, slice(0, 2))
         deal_scale_bytes(nc.gpsimd, w1s, w1s_raw, slice(2, PACK))
         deal_fp4_words(nc.gpsimd, w3q, w3_raw)
-        deal_scale_bytes(nc.gpsimd, w3s, w3s_raw, slice(0, PACK))
 
         xs = keep.tile([P, S], U8, name="xs", align_bytes=64)
         nc.vector.tensor_copy(xs[:], xs_all[:].indirect(offs_sb[:]))
@@ -153,15 +152,24 @@ def tile_picked_tourney_none_po_kernel(
         w2s = keep.tile([P, H], U8, name="w2s", align_bytes=64)
 
         sr01 = keep.tile([P, 2, V], F32, name="sr01", tag="w2_raw", align_bytes=64)
-        sr23 = keep.tile([P, 2, V], F32, name="sr23", align_bytes=64)
+        sr23 = keep.tile([P, 2, V], F32, name="sr23", tag="sr23", align_bytes=64)
         s_right = [sr01[:, 0, :], sr01[:, 1, :], sr23[:, 0, :], sr23[:, 1, :]]
+        w3s = keep.tile([P, N], U8, name="w3s", tag="sr23", align_bytes=64)
         val_rows = [keep.tile([P, S], F32, name=f"val{t}", align_bytes=64) for t in range(PACK)]
         diff = keep.tile([P, PACK, V], F32, name="diff", tag="w2b", align_bytes=64)
+        first, second = slice(0, HALF), slice(HALF, V)
+
+        def halves(name, tags):
+            return [keep.tile([P, PACK, HALF], F32, name=f"{name}{h}", tag=tags[h], align_bytes=64) for h in range(2)]
+
         q = keep.tile([P, PACK, V], F32, name="q", align_bytes=64)
-        val_right = keep.tile([P, PACK, V], F32, name="val_right", align_bytes=64)
         part_left = keep.tile([P, PACK, V], F32, name="part_left", align_bytes=64)
-        part_right = keep.tile([P, PACK, V], F32, name="part_right", align_bytes=64)
-        first, second = slice(0, 2 * BLOCK), slice(2 * BLOCK, V)
+        val_right_tiles = halves("val_right", ("vr0", "vr1"))
+        part_right_tiles = halves("part_right", ("pr0", "pr0"))
+
+        def part(tiles_by_half, tiles, pairs):
+            h = pairs.start // HALF
+            return tiles_by_half[h][:, tiles, pairs.start - h * HALF : pairs.stop - h * HALF]
 
         def entries(lists, pairs):
             return lists[:, pairs.start // GROUP : pairs.stop // GROUP]
@@ -179,8 +187,8 @@ def tile_picked_tourney_none_po_kernel(
         def difference(t):
             nc.vector.tensor_tensor(diff[:, t, :], s_rows[t][:].indirect(left_sb[:]), s_right[t], ALU.subtract)
 
-        def values(t, copy):
-            for h in range(S // BANK):
+        def values(t, *copies):
+            for h, copy in enumerate(copies):
                 cols = slice(h * BANK, (h + 1) * BANK)
                 acc = banks.tile([P, BANK], F32, name="val_bank", tag="bank")
                 times_x(acc[:], w2q[:, P * t : P * (t + 1)].bitcast(FP8X4), w2s[:, P * t : P * (t + 1)], cols)
@@ -190,20 +198,22 @@ def tile_picked_tourney_none_po_kernel(
             nc.scalar.activation(q[:, tiles, pairs], diff[:, tiles, pairs], SIGMOID)
 
         def right_values(t, pairs):
-            nc.scalar.activation(val_right[:, t, pairs], val_rows[t][:].indirect(entries(right_sb, pairs)), COPY)
+            nc.scalar.activation(part(val_right_tiles, t, pairs), val_rows[t][:].indirect(entries(right_sb, pairs)), COPY)
 
         def left_part(t, pairs):
             nc.vector.tensor_tensor(
-                part_left[:, t, pairs], val_rows[t][:].indirect(entries(left_sb, pairs)), q[:, t, pairs], ALU.mult
+                part_left[:, t, pairs], val_rows[t][:].indirect(entries(left_sb, pairs)),
+                q[:, t, pairs], ALU.mult,
             )
 
         def right_part(tiles, pairs):
             nc.vector.scalar_tensor_tensor(
-                part_right[:, tiles, pairs], q[:, tiles, pairs], 1.0, val_right[:, tiles, pairs],
+                part(part_right_tiles, tiles, pairs), q[:, tiles, pairs], 1.0,
+                part(val_right_tiles, tiles, pairs),
                 ALU.subtract, ALU.mult,
             )
 
-        yq = keep.tile([P, V], U32, name="yq", align_bytes=64)
+        yq = keep.tile([P, V], U32, name="yq", tag="pr0", align_bytes=64)
         ys = keep.tile([P, V], U8, name="ys", align_bytes=64)
         out_rows = out_0.rearrange("(p t) v -> p t v", t=PACK)
         out_words = out_1[0].rearrange("p n t -> p (n t)").bitcast(I32)
@@ -211,7 +221,8 @@ def tile_picked_tourney_none_po_kernel(
         def mix(c):
             zb = keep.tile([P, BLOCK * PACK], BF16, name=f"zb{c}", align_bytes=64)
             nc.vector.tensor_tensor(
-                interleaved(zb[:]), by_row_tile(part_left[:, :, block(c)]), by_row_tile(part_right[:, :, block(c)]),
+                interleaved(zb[:]), by_row_tile(part_left[:, :, block(c)]),
+                by_row_tile(part(part_right_tiles, slice(0, PACK), block(c))),
                 ALU.subtract,
             )
             return zb
@@ -254,6 +265,7 @@ def tile_picked_tourney_none_po_kernel(
         def quantize_y(yb, c):
             nc.vector.quantize_mx(out=yq[:, block(c)].bitcast(FP8X4), scales=ys[:, block(c)], in_=yb[:])
 
+        every = slice(0, V)
         right_scores_vector(0)
         nc.vector.quantize_mx(out=w2q[:].bitcast(FP8X4), scales=w2s[:], in_=w2b[:])
         right_scores_vector(1)
@@ -262,48 +274,43 @@ def tile_picked_tourney_none_po_kernel(
         difference(0)
         right_scores_scalar(2)
         difference(1)
-        values(0, nc.scalar.copy)
         right_scores_scalar(3)
+        values(0, nc.scalar.copy, nc.scalar.copy)
         difference(2)
-        values(1, nc.scalar.copy)
+        values(1, nc.scalar.copy, nc.scalar.copy)
         difference(3)
-        gate(slice(0, 2), first)
-        values(2, nc.scalar.copy)
-        left_part(0, first)
-        left_part(1, first)
-        gate(slice(2, PACK), first)
-        values(3, nc.vector.tensor_copy)
+        deal_scale_bytes(nc.gpsimd, w3s, w3s_raw, slice(0, PACK))
+        gate(slice(0, 2), every)
+        values(2, nc.vector.tensor_copy, nc.scalar.copy)
+        left_part(0, every)
+        left_part(1, every)
+        gate(slice(2, PACK), every)
+        values(3, nc.scalar.copy, nc.scalar.copy)
+        left_part(2, every)
         for t in range(PACK):
             right_values(t, first)
-        left_part(2, first)
-        left_part(3, first)
+        left_part(3, every)
         right_part(slice(0, 2), first)
         right_part(slice(2, PACK), first)
-        gate(slice(0, PACK), second)
         zb01 = [mix(c) for c in range(2)]
         z01 = [quantize_z(zb01[c], c) for c in range(2)]
         for t in range(PACK):
             right_values(t, second)
-        left_part(0, second)
-        left_part(1, second)
-        left_part(2, block(2))
-        left_part(3, block(2))
+        right_part(slice(0, 2), second)
+        right_part(slice(2, PACK), block(2))
         yb01 = []
         for c in range(2):
             acc = last_layer(z01[c])
-            yb01.append(round_from_bank(acc, c))
             store_rows(acc, c)
-        right_part(slice(0, 2), second)
-        right_part(slice(2, PACK), second)
+            yb01.append(round_from_bank(acc, c))
+        right_part(slice(2, PACK), block(3))
         zb2 = mix(2)
-        left_part(2, block(3))
-        y2 = store_rows(last_layer(quantize_z(zb2, 2)), 2)
-        left_part(3, block(3))
-        quantize_y(yb01[0], 0)
         zb3 = mix(3)
+        y2 = store_rows(last_layer(quantize_z(zb2, 2)), 2)
+        z3 = quantize_z(zb3, 3)
+        quantize_y(yb01[0], 0)
         quantize_y(yb01[1], 1)
         nc.sync.dma_start(out=out_words[:, first], in_=yq[:, first].bitcast(I32))
-        z3 = quantize_z(zb3, 3)
 
         y3 = keep.tile([P, PACK, BLOCK], F32, name="y3")
         for u in range(2):

@@ -41,6 +41,13 @@ def deal_fp4_words(engine, dealt, raw):
     )
 
 
+def deal_fp4_words_scalar(nc, dealt, raw):
+    nc.scalar.copy(
+        dealt[:].bitcast(U16).rearrange("p (t m) -> p t m", t=PACK),
+        raw[:].bitcast(U16).rearrange("p (m t) -> p t m", t=PACK),
+    )
+
+
 def deal_scale_bytes(engine, dealt, raw, tiles):
     engine.tensor_copy(
         out=dealt[:].rearrange("p (t m) -> p t m", t=PACK)[:, tiles],
@@ -80,18 +87,17 @@ def tile_picked_tourney_none_po_kernel(
         w2_raw = keep.tile([P, PACK, H], F32, name="w2_raw", tag="w2_raw", align_bytes=64)
         warm = keep.tile([P, 2], F32, name="warm")
 
-        nc.vector.memset(xs_all[:, : T // 2].bitcast(I32), 0)
-        nc.gpsimd.memset(xs_all[:, T // 2 :].bitcast(I32), 0)
+        nc.gpsimd.memset(xs_all[:].bitcast(I32), 0)
         nc.vector.memset(warm[:, 0:1], 0.0)
         nc.vector.memset(w1s_raw[:].bitcast(I32), 0)
         nc.vector.memset(w3s_raw[:].bitcast(I32), 0)
 
         nc.sync.dma_start(offs_sb[:], offs)
         nc.scalar.dma_start(out=w1_raw[:].bitcast(I32), in_=w1_words[0].bitcast(I32))
+        nc.sync.dma_start(out=w3_raw[:].bitcast(I32), in_=w3_words[0].bitcast(I32))
         load_scale_rows([nc.sync] * 4, xs_all, x_scales)
         nc.sync.dma_start(out=xw_all[:], in_=x_words[0].rearrange("p n t -> p (n t)").bitcast(I32))
         load_scale_rows([nc.sync] * 3 + [nc.gpsimd], w1s_raw, w1_scales)
-        nc.sync.dma_start(out=w3_raw[:].bitcast(I32), in_=w3_words[0].bitcast(I32))
         nc.sync.dma_start(right_sb[:], right)
         nc.sync.dma_start(out=w2_raw[:], in_=w2.rearrange("(p j) c -> p j c", j=PACK))
         nc.sync.dma_start(left_sb[:], left)
@@ -104,7 +110,7 @@ def tile_picked_tourney_none_po_kernel(
         deal_fp4_words(nc.vector, w1q, w1_raw)
         deal_scale_bytes(nc.gpsimd, w1s, w1s_raw, slice(0, 2))
         deal_scale_bytes(nc.gpsimd, w1s, w1s_raw, slice(2, PACK))
-        deal_fp4_words(nc.gpsimd, w3q, w3_raw)
+        deal_fp4_words_scalar(nc, w3q, w3_raw)
 
         xs = keep.tile([P, S], U8, name="xs", align_bytes=64)
         nc.vector.tensor_copy(xs[:], xs_all[:].indirect(offs_sb[:]))

@@ -59,12 +59,12 @@ def block(c):
     return slice(c * BLOCK, (c + 1) * BLOCK)
 
 
-def interleaved(tile):
-    return tile.rearrange("p (c i t) -> p c t i", i=4, t=PACK)
+def interleaved(tile, run):
+    return tile.rearrange("p (c i t) -> p c t i", i=run, t=PACK)
 
 
-def by_row_tile(tile):
-    return tile.rearrange("p t (c i) -> p c t i", i=4)
+def by_row_tile(tile, run):
+    return tile.rearrange("p t (c i) -> p c t i", i=run)
 
 
 def tile_picked_tourney_none_po_kernel(
@@ -131,17 +131,12 @@ def tile_picked_tourney_none_po_kernel(
             times_x(acc, w1q[:, 2 * P * t : 2 * P * (t + 1)].bitcast(FP4X4), w1s[:, P * t : P * (t + 1)], cols)
 
         s_rows = [keep.tile([P, S], F32, name=f"s{t}", align_bytes=64) for t in range(PACK)]
-        for j in range(S // PIECE - 1):
+        for j in range(S // PIECE):
             cols = slice(j * PIECE, (j + 1) * PIECE)
-            acc = banks.tile([P, 2, PIECE], F32, name="s_shared", tag="bank")
             for t in range(2):
-                score(acc[:, t, :], t, cols)
-            for t in range(2):
-                nc.scalar.copy(s_rows[t][:, cols], acc[:, t, :])
-        for t in range(2):
-            acc = banks.tile([P, PIECE], F32, name="s_own", tag="bank")
-            score(acc[:], t, slice(S - PIECE, S))
-            nc.scalar.copy(s_rows[t][:, S - PIECE :], acc[:])
+                acc = banks.tile([P, PIECE], F32, name="s_own", tag="bank")
+                score(acc[:], t, cols)
+                nc.scalar.copy(s_rows[t][:, cols], acc[:])
 
         s_banks = {}
         for t in (2, 3):
@@ -219,7 +214,7 @@ def tile_picked_tourney_none_po_kernel(
                 ALU.subtract, ALU.mult,
             )
 
-        yq = keep.tile([P, V], U32, name="yq", tag="pr0", align_bytes=64)
+        yq = keep.tile([P, V], U32, name="yq", tag="vr1", align_bytes=64)
         ys = keep.tile([P, V], U8, name="ys", align_bytes=64)
         out_rows = out_0.rearrange("(p t) v -> p t v", t=PACK)
         out_words = out_1[0].rearrange("p n t -> p (n t)").bitcast(I32)
@@ -227,8 +222,8 @@ def tile_picked_tourney_none_po_kernel(
         def mix(c):
             zb = keep.tile([P, BLOCK * PACK], BF16, name=f"zb{c}", align_bytes=64)
             nc.vector.tensor_tensor(
-                interleaved(zb[:]), by_row_tile(part_left[:, :, block(c)]),
-                by_row_tile(part(part_right_tiles, slice(0, PACK), block(c))),
+                interleaved(zb[:], 2), by_row_tile(part_left[:, :, block(c)], 2),
+                by_row_tile(part(part_right_tiles, slice(0, PACK), block(c)), 2),
                 ALU.subtract,
             )
             return zb
@@ -253,13 +248,13 @@ def tile_picked_tourney_none_po_kernel(
             return acc
 
         def round_from_bank(acc, c):
-            yb = keep.tile([P, BLOCK * PACK], BF16, name=f"yb{c}", align_bytes=64)
+            yb = keep.tile([P, BLOCK * PACK], BF16, name=f"yb{c}", tag=f"yb{c}", align_bytes=64)
             nc.scalar.copy(yb[:].rearrange("p (n t) -> p n t", t=PACK), acc[:].rearrange("p t n -> p n t"))
             return yb
 
         def round_from_rows(y, c):
             yb = keep.tile([P, BLOCK * PACK], BF16, name=f"yb{c}", align_bytes=64)
-            nc.vector.tensor_copy(interleaved(yb[:]), by_row_tile(y[:]))
+            nc.vector.tensor_copy(interleaved(yb[:], 4), by_row_tile(y[:], 4))
             return yb
 
         def store_rows(acc, c):
@@ -297,36 +292,44 @@ def tile_picked_tourney_none_po_kernel(
             right_values(t, first)
         left_part(3, every)
         right_part(slice(0, 2), first)
-        right_part(slice(2, PACK), first)
+        for c in range(2):
+            right_part(slice(2, PACK), block(c))
         zb01 = [mix(c) for c in range(2)]
         z01 = [quantize_z(zb01[c], c) for c in range(2)]
         for t in range(PACK):
             right_values(t, second)
-        right_part(slice(0, 2), second)
-        right_part(slice(2, PACK), block(2))
-        yb01 = []
+        low, high = slice(0, 2), slice(2, PACK)
+        right_part(low, block(2))
+        acc01 = [last_layer(z01[c]) for c in range(2)]
         for c in range(2):
-            acc = last_layer(z01[c])
-            store_rows(acc, c)
-            yb01.append(round_from_bank(acc, c))
-        right_part(slice(2, PACK), block(3))
+            store_rows(acc01[c], c)
+        yb01 = [round_from_bank(acc01[c], c) for c in range(2)]
+        right_part(high, block(2))
+        right_part(low, block(3))
         zb2 = mix(2)
-        zb3 = mix(3)
+        right_part(high, block(3))
         y2 = store_rows(last_layer(quantize_z(zb2, 2)), 2)
-        z3 = quantize_z(zb3, 3)
+        zb3 = mix(3)
         quantize_y(yb01[0], 0)
+        z3 = quantize_z(zb3, 3)
         quantize_y(yb01[1], 1)
         nc.sync.dma_start(out=out_words[:, first], in_=yq[:, first].bitcast(I32))
+        yb2 = round_from_rows(y2, 2)
 
         y3 = keep.tile([P, PACK, BLOCK], F32, name="y3")
-        for u in range(2):
+
+        def last_rows(tiles, copy):
             acc = banks.tile([P, 2, BLOCK], F32, name="y3_bank", tag="bank")
             for e in range(2):
-                times_w3(acc[:, e, :], 2 * u + e, z3)
-            nc.scalar.copy(y3[:, 2 * u : 2 * u + 2, :], acc[:])
+                times_w3(acc[:, e, :], tiles.start + e, z3)
+            copy(y3[:, tiles, :], acc[:])
+
+        last_rows(low, nc.scalar.copy)
+        yb3 = round_from_bank(last_layer(z3), 3)
+        last_rows(high, nc.vector.tensor_copy)
         nc.sync.dma_start(out=out_rows[:, :, block(3)], in_=y3[:])
-        quantize_y(round_from_rows(y2, 2), 2)
-        quantize_y(round_from_rows(y3, 3), 3)
+        quantize_y(yb2, 2)
+        quantize_y(yb3, 3)
         nc.sync.dma_start(out=out_words[:, second], in_=yq[:, second].bitcast(I32))
         for quad in range(4):
             queue = nc.sync if quad % 2 == 0 else nc.scalar

@@ -84,7 +84,7 @@ def tile_picked_tourney_none_po_kernel(
         w1s_raw = keep.tile([P, H], U8, name="w1s_raw", align_bytes=64)
         w3_raw = keep.tile([P, 2 * N], U8, name="w3_raw", align_bytes=64)
         w3s_raw = keep.tile([P, N], U8, name="w3s_raw", tag="w3s_raw", align_bytes=64)
-        w2_raw = keep.tile([P, PACK, H], F32, name="w2_raw", tag="w2_raw", align_bytes=64)
+        w2_raw = keep.tile([P, PACK, H], F32, name="w2_raw", align_bytes=64)
         warm = keep.tile([P, 2], F32, name="warm")
 
         nc.gpsimd.memset(xs_all[:].bitcast(I32), 0)
@@ -98,8 +98,8 @@ def tile_picked_tourney_none_po_kernel(
         load_scale_rows([nc.sync] * 4, xs_all, x_scales)
         nc.sync.dma_start(out=xw_all[:], in_=x_words[0].rearrange("p n t -> p (n t)").bitcast(I32))
         load_scale_rows([nc.sync] * 3 + [nc.gpsimd], w1s_raw, w1_scales)
-        nc.sync.dma_start(right_sb[:], right)
         nc.sync.dma_start(out=w2_raw[:], in_=w2.rearrange("(p j) c -> p j c", j=PACK))
+        nc.sync.dma_start(right_sb[:], right)
         nc.sync.dma_start(left_sb[:], left)
         load_scale_rows([nc.sync] * 4, w3s_raw, w3_scales)
         nc.scalar.activation(warm[:, 1:2], warm[:, 0:1], SIGMOID)
@@ -152,7 +152,7 @@ def tile_picked_tourney_none_po_kernel(
         w2q = keep.tile([P, H], U32, name="w2q", align_bytes=64)
         w2s = keep.tile([P, H], U8, name="w2s", align_bytes=64)
 
-        sr01 = keep.tile([P, 2, V], F32, name="sr01", tag="w2_raw", align_bytes=64)
+        sr01 = keep.tile([P, 2, V], F32, name="sr01", align_bytes=64)
         sr23 = keep.tile([P, 2, V], F32, name="sr23", tag="sr23", align_bytes=64)
         s_right = [sr01[:, 0, :], sr01[:, 1, :], sr23[:, 0, :], sr23[:, 1, :]]
         w3s = keep.tile([P, N], U8, name="w3s", tag="sr23", align_bytes=64)
@@ -222,8 +222,8 @@ def tile_picked_tourney_none_po_kernel(
         def mix(c):
             zb = keep.tile([P, BLOCK * PACK], BF16, name=f"zb{c}", align_bytes=64)
             nc.vector.tensor_tensor(
-                interleaved(zb[:], 2), by_row_tile(part_left[:, :, block(c)], 2),
-                by_row_tile(part(part_right_tiles, slice(0, PACK), block(c)), 2),
+                interleaved(zb[:], 4), by_row_tile(part_left[:, :, block(c)], 4),
+                by_row_tile(part(part_right_tiles, slice(0, PACK), block(c)), 4),
                 ALU.subtract,
             )
             return zb
@@ -325,11 +325,10 @@ def tile_picked_tourney_none_po_kernel(
             copy(y3[:, tiles, :], acc[:])
 
         last_rows(low, nc.scalar.copy)
-        yb3 = round_from_bank(last_layer(z3), 3)
-        last_rows(high, nc.vector.tensor_copy)
+        last_rows(high, nc.scalar.copy)
         nc.sync.dma_start(out=out_rows[:, :, block(3)], in_=y3[:])
         quantize_y(yb2, 2)
-        quantize_y(yb3, 3)
+        quantize_y(round_from_rows(y3, 3), 3)
         nc.sync.dma_start(out=out_words[:, second], in_=yq[:, second].bitcast(I32))
         for quad in range(4):
             queue = nc.sync if quad % 2 == 0 else nc.scalar

@@ -260,7 +260,7 @@ def tile_picked_tourney_none_po_kernel(
         def store_rows(acc, c):
             y = keep.tile([P, PACK, BLOCK], F32, name=f"y{c}")
             nc.scalar.copy(y[:], acc[:])
-            nc.sync.dma_start(out=out_rows[:, :, block(c)], in_=y[:])
+            (nc.scalar if c == 1 else nc.sync).dma_start(out=out_rows[:, :, block(c)], in_=y[:])
             return y
 
         def quantize_y(yb, c):
@@ -326,7 +326,7 @@ def tile_picked_tourney_none_po_kernel(
 
         last_rows(low, nc.scalar.copy)
         last_rows(high, nc.scalar.copy)
-        nc.sync.dma_start(out=out_rows[:, :, block(3)], in_=y3[:])
+        nc.scalar.dma_start(out=out_rows[:, :, block(3)], in_=y3[:])
         quantize_y(yb2, 2)
         quantize_y(round_from_rows(y3, 3), 3)
         nc.sync.dma_start(out=out_words[:, second], in_=yq[:, second].bitcast(I32))

@@ -280,7 +280,7 @@ def tile_picked_tourney_none_po_kernel(
         difference(2)
         values(1, nc.scalar.copy, nc.scalar.copy)
         difference(3)
-        deal_scale_bytes(nc.gpsimd, w3s, w3s_raw, slice(0, PACK))
+        deal_scale_bytes(nc.vector, w3s, w3s_raw, slice(0, PACK))
         gate(slice(0, 2), every)
         values(2, nc.vector.tensor_copy, nc.scalar.copy)
         left_part(0, every)

@@ -155,7 +155,7 @@ def tile_picked_tourney_none_po_kernel(
         sr01 = keep.tile([P, 2, V], F32, name="sr01", align_bytes=64)
         sr23 = keep.tile([P, 2, V], F32, name="sr23", tag="sr23", align_bytes=64)
         s_right = [sr01[:, 0, :], sr01[:, 1, :], sr23[:, 0, :], sr23[:, 1, :]]
-        w3s = keep.tile([P, N], U8, name="w3s", tag="sr23", align_bytes=64)
+        w3s = keep.tile([P, N], U8, name="w3s", align_bytes=64)
         val_rows = [keep.tile([P, S], F32, name=f"val{t}", align_bytes=64) for t in range(PACK)]
         diff = keep.tile([P, PACK, V], F32, name="diff", tag="w2b", align_bytes=64)
         first, second = slice(0, HALF), slice(HALF, V)
@@ -269,6 +269,7 @@ def tile_picked_tourney_none_po_kernel(
         every = slice(0, V)
         right_scores_vector(0)
         nc.vector.quantize_mx(out=w2q[:].bitcast(FP8X4), scales=w2s[:], in_=w2b[:])
+        deal_scale_bytes(nc.vector, w3s, w3s_raw, slice(0, PACK))
         right_scores_vector(1)
         copy_scores(2)
         copy_scores(3)
@@ -280,9 +281,8 @@ def tile_picked_tourney_none_po_kernel(
         difference(2)
         values(1, nc.scalar.copy, nc.scalar.copy)
         difference(3)
-        deal_scale_bytes(nc.vector, w3s, w3s_raw, slice(0, PACK))
         gate(slice(0, 2), every)
-        values(2, nc.vector.tensor_copy, nc.scalar.copy)
+        values(2, nc.scalar.copy, nc.scalar.copy)
         left_part(0, every)
         left_part(1, every)
         gate(slice(2, PACK), every)

@@ -188,10 +188,12 @@ def tile_picked_tourney_none_po_kernel(
         def difference(t):
             nc.vector.tensor_tensor(diff[:, t, :], s_rows[t][:].indirect(left_sb[:]), s_right[t], ALU.subtract)
 
-        def values(t, *copies):
-            for h, copy in enumerate(copies):
-                cols = slice(h * BANK, (h + 1) * BANK)
-                acc = banks.tile([P, BANK], F32, name="val_bank", tag="bank")
+        def values(t, *shares):
+            start = 0
+            for width, copy in shares:
+                cols = slice(start, start + width)
+                start += width
+                acc = banks.tile([P, width], F32, name="val_bank", tag="bank")
                 times_x(acc[:], w2q[:, P * t : P * (t + 1)].bitcast(FP8X4), w2s[:, P * t : P * (t + 1)], cols)
                 copy(val_rows[t][:, cols], acc[:])
 
@@ -267,6 +269,7 @@ def tile_picked_tourney_none_po_kernel(
             nc.vector.quantize_mx(out=yq[:, block(c)].bitcast(FP8X4), scales=ys[:, block(c)], in_=yb[:])
 
         every = slice(0, V)
+        on_scalar = [(BANK, nc.scalar.copy)] * 2
         right_scores_vector(0)
         nc.vector.quantize_mx(out=w2q[:].bitcast(FP8X4), scales=w2s[:], in_=w2b[:])
         deal_scale_bytes(nc.vector, w3s, w3s_raw, slice(0, PACK))
@@ -277,16 +280,16 @@ def tile_picked_tourney_none_po_kernel(
         right_scores_scalar(2)
         difference(1)
         right_scores_scalar(3)
-        values(0, nc.scalar.copy, nc.scalar.copy)
+        values(0, *on_scalar)
         difference(2)
-        values(1, nc.scalar.copy, nc.scalar.copy)
+        values(1, *on_scalar)
         difference(3)
         gate(slice(0, 2), every)
-        values(2, nc.scalar.copy, nc.scalar.copy)
+        values(2, (PIECE, nc.vector.tensor_copy), (PIECE, nc.scalar.copy), (BANK, nc.scalar.copy))
         left_part(0, every)
         left_part(1, every)
         gate(slice(2, PACK), every)
-        values(3, nc.scalar.copy, nc.scalar.copy)
+        values(3, *on_scalar)
         left_part(2, every)
         for t in range(PACK):
             right_values(t, first)

from contextlib import ExitStack

import concourse.mybir as mybir

K, T, S, V, N, H = 512, 2048, 1024, 512, 512, 512
FLOPS = 2 * K * H * S * 2 + 2 * H * N * V

F32 = mybir.dt.float32
BF16 = mybir.dt.bfloat16
I32 = mybir.dt.int32
U32 = mybir.dt.uint32
U16 = mybir.dt.uint16
U8 = mybir.dt.uint8
FP8X4 = mybir.dt.float8_e4m3fn_x4
FP4X4 = mybir.dt.float4_e2m1fn_x4
ALU = mybir.AluOpType
SIGMOID = mybir.ActivationFunctionType.Sigmoid
COPY = mybir.ActivationFunctionType.Copy

P = 128
PACK = 4
GROUP = 16
BANK = 512
PIECE = 256
HALF = 256
BLOCK = 128


def load_scale_rows(queues, plane, scales):
    for quad, queue in enumerate(queues):
        queue.dma_start(
            out=plane[32 * quad : 32 * quad + 4, :].bitcast(I32),
            in_=scales[0, 4 * quad : 4 * quad + 4, :].bitcast(I32),
        )


def deal_fp4_words(engine, dealt, raw):
    engine.tensor_copy(
        out=dealt[:].rearrange("p (t m b) -> p t m b", t=PACK, b=2),
        in_=raw[:].rearrange("p (m t b) -> p t m b", t=PACK, b=2),
    )


def deal_fp4_words_scalar(nc, dealt, raw):
    nc.scalar.copy(
        dealt[:].bitcast(U16).rearrange("p (t m) -> p t m", t=PACK),
        raw[:].bitcast(U16).rearrange("p (m t) -> p t m", t=PACK),
    )


def deal_scale_bytes(engine, dealt, raw, tiles):
    engine.tensor_copy(
        out=dealt[:].rearrange("p (t m) -> p t m", t=PACK)[:, tiles],
        in_=raw[:].rearrange("p (m t) -> p t m", t=PACK)[:, tiles],
    )


def block(c):
    return slice(c * BLOCK, (c + 1) * BLOCK)


def interleaved(tile, run):
    return tile.rearrange("p (c i t) -> p c t i", i=run, t=PACK)


def by_row_tile(tile, run):
    return tile.rearrange("p t (c i) -> p c t i", i=run)


def tile_picked_tourney_none_po_kernel(
    tc, x_words, x_scales, w1_words, w1_scales, w2, w3_words, w3_scales, offs, left, right, out_0, out_1, out_2
):
    nc = tc.nc
    with ExitStack() as ctx:
        keep = ctx.enter_context(tc.tile_pool(name="keep", bufs=1))
        banks = ctx.enter_context(tc.psum_pool(name="banks", bufs=8))

        offs_sb = keep.tile([P, S // GROUP], U16, name="offs_sb")
        left_sb = keep.tile([P, V // GROUP], U16, name="left_sb")
        right_sb = keep.tile([P, V // GROUP], U16, name="right_sb")
        xs_all = keep.tile([P, T], U8, name="xs_all", align_bytes=64)
        xw_all = keep.tile([P, T], I32, name="xw_all", align_bytes=64)
        w1_raw = keep.tile([P, 2 * H], U8, name="w1_raw", align_bytes=64)
        w1s_raw = keep.tile([P, H], U8, name="w1s_raw", align_bytes=64)
        w3_raw = keep.tile([P, 2 * N], U8, name="w3_raw", align_bytes=64)
        w3s_raw = keep.tile([P, N], U8, name="w3s_raw", tag="w3s_raw", align_bytes=64)
        w2_raw = keep.tile([P, PACK, H], F32, name="w2_raw", align_bytes=64)
        warm = keep.tile([P, 2], F32, name="warm")

        nc.gpsimd.memset(xs_all[:].bitcast(I32), 0)
        nc.vector.memset(warm[:, 0:1], 0.0)
        nc.vector.memset(w1s_raw[:].bitcast(I32), 0)
        nc.vector.memset(w3s_raw[:].bitcast(I32), 0)

        nc.sync.dma_start(offs_sb[:], offs)
        nc.scalar.dma_start(out=w1_raw[:].bitcast(I32), in_=w1_words[0].bitcast(I32))
        nc.sync.dma_start(out=w3_raw[:].bitcast(I32), in_=w3_words[0].bitcast(I32))
        load_scale_rows([nc.sync] * 4, xs_all, x_scales)
        nc.sync.dma_start(out=xw_all[:], in_=x_words[0].rearrange("p n t -> p (n t)").bitcast(I32))
        load_scale_rows([nc.sync] * 3 + [nc.gpsimd], w1s_raw, w1_scales)
        nc.sync.dma_start(out=w2_raw[:], in_=w2.rearrange("(p j) c -> p j c", j=PACK))
        nc.sync.dma_start(right_sb[:], right)
        nc.sync.dma_start(left_sb[:], left)
        load_scale_rows([nc.sync] * 4, w3s_raw, w3_scales)
        nc.scalar.activation(warm[:, 1:2], warm[:, 0:1], SIGMOID)

        w1q = keep.tile([P, 2 * H], U8, name="w1q", align_bytes=64)
        w1s = keep.tile([P, H], U8, name="w1s", align_bytes=64)
        w3q = keep.tile([P, 2 * N], U8, name="w3q", align_bytes=64)
        deal_fp4_words(nc.vector, w1q, w1_raw)
        deal_scale_bytes(nc.gpsimd, w1s, w1s_raw, slice(0, 2))
        deal_scale_bytes(nc.gpsimd, w1s, w1s_raw, slice(2, PACK))
        deal_fp4_words_scalar(nc, w3q, w3_raw)

        xs = keep.tile([P, S], U8, name="xs", align_bytes=64)
        nc.vector.tensor_copy(xs[:], xs_all[:].indirect(offs_sb[:]))
        xw = keep.tile([P, S], U32, name="xw", align_bytes=64)
        for j in range(S // PIECE):
            nc.vector.tensor_copy(
                xw[:, j * PIECE : (j + 1) * PIECE],
                xw_all[:].bitcast(U32).indirect(offs_sb[:, j * PIECE // GROUP : (j + 1) * PIECE // GROUP]),
            )

        def times_x(acc, lhs, lhs_scale, cols):
            nc.tensor.matmul_mx(
                out=acc, lhsT=lhs, lhsT_scale=lhs_scale,
                rhs=xw[:, cols].bitcast(FP8X4), rhs_scale=xs[:, cols], start=True, stop=True,
            )

        def score(acc, t, cols):
            times_x(acc, w1q[:, 2 * P * t : 2 * P * (t + 1)].bitcast(FP4X4), w1s[:, P * t : P * (t + 1)], cols)

        s_rows = [keep.tile([P, S], F32, name=f"s{t}", align_bytes=64) for t in range(PACK)]
        for j in range(S // PIECE):
            cols = slice(j * PIECE, (j + 1) * PIECE)
            for t in range(2):
                acc = banks.tile([P, PIECE], F32, name="s_own", tag="bank")
                score(acc[:], t, cols)
                nc.scalar.copy(s_rows[t][:, cols], acc[:])

        s_banks = {}
        for t in (2, 3):
            for h in range(S // BANK):
                s_banks[t, h] = banks.tile([P, BANK], F32, name=f"s_bank{t}{h}", tag="bank")
                score(s_banks[t, h][:], t, slice(h * BANK, (h + 1) * BANK))

        w2b = keep.tile([P, H * PACK], BF16, name="w2b", tag="w2b", align_bytes=64)
        nc.vector.tensor_copy(
            w2b[:].rearrange("p (t m j) -> p m j t", t=PACK, j=PACK),
            w2_raw[:].rearrange("p j (m t) -> p m j t", t=PACK),
        )
        w2q = keep.tile([P, H], U32, name="w2q", align_bytes=64)
        w2s = keep.tile([P, H], U8, name="w2s", align_bytes=64)

        sr01 = keep.tile([P, 2, V], F32, name="sr01", align_bytes=64)
        sr23 = keep.tile([P, 2, V], F32, name="sr23", tag="sr23", align_bytes=64)
        s_right = [sr01[:, 0, :], sr01[:, 1, :], sr23[:, 0, :], sr23[:, 1, :]]
        w3s = keep.tile([P, N], U8, name="w3s", align_bytes=64)
        val_rows = [keep.tile([P, S], F32, name=f"val{t}", align_bytes=64) for t in range(PACK)]
        diff = keep.tile([P, PACK, V], F32, name="diff", tag="w2b", align_bytes=64)
        first, second = slice(0, HALF), slice(HALF, V)

        def halves(name, tags):
            return [keep.tile([P, PACK, HALF], F32, name=f"{name}{h}", tag=tags[h], align_bytes=64) for h in range(2)]

        q = keep.tile([P, PACK, V], F32, name="q", align_bytes=64)
        part_left = keep.tile([P, PACK, V], F32, name="part_left", align_bytes=64)
        val_right_tiles = halves("val_right", ("vr0", "vr1"))
        part_right_tiles = halves("part_right", ("pr0", "pr0"))

        def part(tiles_by_half, tiles, pairs):
            h = pairs.start // HALF
            return tiles_by_half[h][:, tiles, pairs.start - h * HALF : pairs.stop - h * HALF]

        def entries(lists, pairs):
            return lists[:, pairs.start // GROUP : pairs.stop // GROUP]

        def copy_scores(t):
            for h in range(S // BANK):
                nc.scalar.copy(s_rows[t][:, h * BANK : (h + 1) * BANK], s_banks[t, h][:])

        def right_scores_vector(t):
            nc.vector.tensor_copy(s_right[t], s_rows[t][:].indirect(right_sb[:]))

        def right_scores_scalar(t):
            nc.scalar.activation(s_right[t], s_rows[t][:].indirect(right_sb[:]), COPY)

        def difference(t):
            nc.vector.tensor_tensor(diff[:, t, :], s_rows[t][:].indirect(left_sb[:]), s_right[t], ALU.subtract)

        def values(t, *shares):
            start = 0
            for width, copy in shares:
                cols = slice(start, start + width)
                start += width
                acc = banks.tile([P, width], F32, name="val_bank", tag="bank")
                times_x(acc[:], w2q[:, P * t : P * (t + 1)].bitcast(FP8X4), w2s[:, P * t : P * (t + 1)], cols)
                copy(val_rows[t][:, cols], acc[:])

        def gate(tiles, pairs):
            nc.scalar.activation(q[:, tiles, pairs], diff[:, tiles, pairs], SIGMOID)

        def right_values(t, pairs):
            nc.scalar.activation(part(val_right_tiles, t, pairs), val_rows[t][:].indirect(entries(right_sb, pairs)), COPY)

        def left_part(t, pairs):
            nc.vector.tensor_tensor(
                part_left[:, t, pairs], val_rows[t][:].indirect(entries(left_sb, pairs)),
                q[:, t, pairs], ALU.mult,
            )

        def right_part(tiles, pairs):
            nc.vector.scalar_tensor_tensor(
                part(part_right_tiles, tiles, pairs), q[:, tiles, pairs], 1.0,
                part(val_right_tiles, tiles, pairs),
                ALU.subtract, ALU.mult,
            )

        yq = keep.tile([P, V], U32, name="yq", tag="vr1", align_bytes=64)
        ys = keep.tile([P, V], U8, name="ys", align_bytes=64)
        out_rows = out_0.rearrange("(p t) v -> p t v", t=PACK)
        out_words = out_1[0].rearrange("p n t -> p (n t)").bitcast(I32)

        def mix(c):
            zb = keep.tile([P, BLOCK * PACK], BF16, name=f"zb{c}", align_bytes=64)
            nc.vector.tensor_tensor(
                interleaved(zb[:], 4), by_row_tile(part_left[:, :, block(c)], 4),
                by_row_tile(part(part_right_tiles, slice(0, PACK), block(c)), 4),
                ALU.subtract,
            )
            return zb

        def quantize_z(zb, c):
            zq = keep.tile([P, BLOCK], U32, name=f"zq{c}", align_bytes=64)
            zs = keep.tile([P, BLOCK], U8, name=f"zs{c}", align_bytes=64)
            nc.vector.quantize_mx(out=zq[:].bitcast(FP8X4), scales=zs[:], in_=zb[:])
            return zq, zs

        def times_w3(acc, t, z):
            nc.tensor.matmul_mx(
                out=acc,
                lhsT=w3q[:, 2 * P * t : 2 * P * (t + 1)].bitcast(FP4X4), lhsT_scale=w3s[:, P * t : P * (t + 1)],
                rhs=z[0][:].bitcast(FP8X4), rhs_scale=z[1][:], start=True, stop=True,
            )

        def last_layer(z):
            acc = banks.tile([P, PACK, BLOCK], F32, name="y_bank", tag="bank")
            for t in range(PACK):
                times_w3(acc[:, t, :], t, z)
            return acc

        def round_from_bank(acc, c):
            yb = keep.tile([P, BLOCK * PACK], BF16, name=f"yb{c}", tag=f"yb{c}", align_bytes=64)
            nc.scalar.copy(yb[:].rearrange("p (n t) -> p n t", t=PACK), acc[:].rearrange("p t n -> p n t"))
            return yb

        def round_from_rows(y, c):
            yb = keep.tile([P, BLOCK * PACK], BF16, name=f"yb{c}", align_bytes=64)
            nc.vector.tensor_copy(interleaved(yb[:], 4), by_row_tile(y[:], 4))
            return yb

        def store_rows(acc, c):
            y = keep.tile([P, PACK, BLOCK], F32, name=f"y{c}")
            nc.scalar.copy(y[:], acc[:])
            (nc.scalar if c == 1 else nc.sync).dma_start(out=out_rows[:, :, block(c)], in_=y[:])
            return y

        def quantize_y(yb, c):
            nc.vector.quantize_mx(out=yq[:, block(c)].bitcast(FP8X4), scales=ys[:, block(c)], in_=yb[:])

        every = slice(0, V)
        on_scalar = [(BANK, nc.scalar.copy)] * 2
        right_scores_vector(0)
        nc.vector.quantize_mx(out=w2q[:].bitcast(FP8X4), scales=w2s[:], in_=w2b[:])
        deal_scale_bytes(nc.vector, w3s, w3s_raw, slice(0, PACK))
        right_scores_vector(1)
        copy_scores(2)
        copy_scores(3)
        difference(0)
        right_scores_scalar(2)
        difference(1)
        right_scores_scalar(3)
        values(0, *on_scalar)
        difference(2)
        values(1, *on_scalar)
        difference(3)
        gate(slice(0, 2), every)
        values(2, (PIECE, nc.vector.tensor_copy), (PIECE, nc.scalar.copy), (BANK, nc.scalar.copy))
        left_part(0, every)
        left_part(1, every)
        gate(slice(2, PACK), every)
        values(3, *on_scalar)
        left_part(2, every)
        for t in range(PACK):
            right_values(t, first)
        left_part(3, every)
        right_part(slice(0, 2), first)
        for c in range(2):
            right_part(slice(2, PACK), block(c))
        zb01 = [mix(c) for c in range(2)]
        z01 = [quantize_z(zb01[c], c) for c in range(2)]
        for t in range(PACK):
            right_values(t, second)
        low, high = slice(0, 2), slice(2, PACK)
        right_part(low, block(2))
        acc01 = [last_layer(z01[c]) for c in range(2)]
        for c in range(2):
            store_rows(acc01[c], c)
        yb01 = [round_from_bank(acc01[c], c) for c in range(2)]
        right_part(high, block(2))
        right_part(low, block(3))
        zb2 = mix(2)
        right_part(high, block(3))
        y2 = store_rows(last_layer(quantize_z(zb2, 2)), 2)
        zb3 = mix(3)
        quantize_y(yb01[0], 0)
        z3 = quantize_z(zb3, 3)
        quantize_y(yb01[1], 1)
        nc.sync.dma_start(out=out_words[:, first], in_=yq[:, first].bitcast(I32))
        yb2 = round_from_rows(y2, 2)

        y3 = keep.tile([P, PACK, BLOCK], F32, name="y3")

        def last_rows(tiles, copy):
            acc = banks.tile([P, 2, BLOCK], F32, name="y3_bank", tag="bank")
            for e in range(2):
                times_w3(acc[:, e, :], tiles.start + e, z3)
            copy(y3[:, tiles, :], acc[:])

        last_rows(low, nc.scalar.copy)
        last_rows(high, nc.scalar.copy)
        nc.scalar.dma_start(out=out_rows[:, :, block(3)], in_=y3[:])
        quantize_y(yb2, 2)
        quantize_y(round_from_rows(y3, 3), 3)
        nc.sync.dma_start(out=out_words[:, second], in_=yq[:, second].bitcast(I32))
        for quad in range(4):
            queue = nc.sync if quad % 2 == 0 else nc.scalar
            queue.dma_start(
                out=out_2[0, 4 * quad : 4 * quad + 4, :].bitcast(I32),
                in_=ys[32 * quad : 32 * quad + 4, :].bitcast(I32),
            )
